import numpy as np
import ml_dtypes


def mxq(x, axis, fmt="e4m3"):
    dtype, down = {"e4m3": (ml_dtypes.float8_e4m3fn, 7), "e5m2": (ml_dtypes.float8_e5m2, 14)}[fmt]
    v = np.moveaxis(np.asarray(x, np.float32).astype(ml_dtypes.bfloat16).astype(np.float64), axis, -1)
    blocks = v.reshape(v.shape[:-1] + (-1, 32))
    amax = np.abs(blocks).max(-1, keepdims=True)
    byte = np.maximum(np.where(amax > 0, np.frexp(amax)[1] - 1 + 127, 0) - down, 1)
    scale = np.exp2(byte - 127.0)
    codes = (blocks / scale).astype(np.float32).astype(dtype).astype(np.float64)
    return np.moveaxis((codes * scale).reshape(v.shape), -1, axis)


WIDE = False


def mx_kscale(k):
    if not WIDE:
        return np.ones(k)
    levels = np.array([10, -10, 5, -5, 0])
    if k % 512:
        return np.exp2(np.random.permutation(np.resize(levels, k // 32))).repeat(32)
    a = np.empty((k // 512, 16))
    for p in range(k // 512):
        a[p, :8] = np.random.permutation(np.resize(levels, 8))
        for g in range(8):
            far = levels[np.abs(levels - a[p, g]) >= 10]
            a[p, g + 8] = far[np.random.randint(len(far))]
    return np.exp2(a.ravel()).repeat(32)


def f64(x):
    return np.asarray(x).astype(np.float64)


def striped(idx):
    return np.tile(idx.reshape(-1, 16).T, (8, 1)).astype(np.uint16)


def unstriped(offs):
    return offs[:16].T.reshape(-1).astype(np.int64)


def striped8(idx):
    return np.concatenate([x.reshape(-1, 16).T for x in idx]).astype(np.uint16)


def runs(offs, k):
    lists = np.stack([offs[16 * r : 16 * r + 16].T.reshape(-1) for r in range(8)]).astype(np.int64)
    return lists[np.arange(k) % 512 // 64]


def pack_weight(w):
    k, n = w.shape
    w = f64(np.asarray(w, np.float32).astype(ml_dtypes.bfloat16)).reshape(k // 32, 32, n)
    amax = np.abs(w).max(1)
    byte = np.clip(np.where(amax > 0, np.frexp(amax)[1] - 1 + 127 - 7, 1), 1, 254)
    scaled = (w * np.exp2(127.0 - byte)[:, None, :]).reshape(k, n).astype(np.float32)
    words = np.ascontiguousarray(scaled.reshape(k // 512, 128, 4, n).transpose(0, 1, 3, 2)).astype(ml_dtypes.float8_e4m3fn).view(np.uint8)
    return words, np.ascontiguousarray(byte.astype(np.uint8).reshape(k // 512, 16, n))


def unpack_weight(words, scales):
    g, p, n, _ = words.shape
    vals = np.ascontiguousarray(words).view(ml_dtypes.float8_e4m3fn).astype(np.float64) * np.repeat(np.exp2(scales.astype(np.float64) - 127.0), 8, axis=1)[..., None]
    return vals.transpose(0, 1, 3, 2).reshape(g * 512, n)


E2M1 = np.array([0.0, 0.5, 1.0, 1.5, 2.0, 3.0, 4.0, 6.0, -0.0, -0.5, -1.0, -1.5, -2.0, -3.0, -4.0, -6.0])


def pack_fp4(w):
    k, n = w.shape
    w = f64(np.asarray(w, np.float32).astype(ml_dtypes.bfloat16)).reshape(k // 32, 32, n)
    amax = np.abs(w).max(1)
    mant, ex = np.frexp(amax / 6.0)
    byte = np.clip(np.where(amax > 0, np.where(mant > 0.5, ex, ex - 1) + 127, 1), 1, 254)
    scaled = (w * np.exp2(127.0 - byte)[:, None, :]).reshape(k, n).astype(np.float32)
    c = np.ascontiguousarray(scaled.reshape(k // 512, 128, 4, n).transpose(0, 1, 3, 2)).astype(ml_dtypes.float4_e2m1fn).view(np.uint8) & 0xF
    words = (c[..., 0::2] | (c[..., 1::2] << 4)).reshape(k // 512, 128, 2 * n)
    return np.ascontiguousarray(words), np.ascontiguousarray(byte.astype(np.uint8).reshape(k // 512, 16, n))


def unpack_fp4(words, scales):
    g, _, n = scales.shape
    words = np.ascontiguousarray(words).reshape(g, 128, n, 2)
    nib = np.empty((g, 128, n, 4), np.uint8)
    nib[..., 0::2] = words & 0xF
    nib[..., 1::2] = words >> 4
    vals = E2M1[nib] * np.repeat(np.exp2(scales.astype(np.float64) - 127.0), 8, axis=1)[..., None]
    return vals.transpose(0, 1, 3, 2).reshape(g * 512, n)


def planes(y):
    n, m = y.shape
    v = y.astype(np.float32).astype(ml_dtypes.bfloat16).astype(np.float64).reshape(n // 32, 32, m)
    top = np.abs(v).max(1)
    byte = np.clip(np.where(top > 0, np.frexp(top)[1] - 1 + 127 - 7, 1), 1, 254)
    codes = (v * np.exp2(127.0 - byte)[:, None, :]).reshape(n, m).astype(np.float32).astype(ml_dtypes.float8_e4m3fn).view(np.uint8)
    words = codes.reshape(n // 512, 128, 4, m).transpose(0, 1, 3, 2)
    return np.ascontiguousarray(words), np.ascontiguousarray(byte.astype(np.uint8).reshape(n // 512, 16, m))


K, T, S, H, C, G = 512, 1024, 512, 512, 512, 2048


def setup_inputs():
    n = np.random.standard_normal
    s = mx_kscale(K)[:, None]
    packed_xT = pack_weight(n((K, T)) * s)
    packed_w1 = pack_fp4(n((K, H)) / np.sqrt(K) / s)
    packed_dT = pack_weight(n((K, G)) / s)
    return {
        "x_words": packed_xT[0],
        "x_scales": packed_xT[1],
        "w1_words": packed_w1[0],
        "w1_scales": packed_w1[1],
        "gs": (np.random.uniform(0.5, 1.5, (K, 1)) / s).astype(np.float32),
        "gk": (np.random.uniform(0.5, 1.5, (K, 1)) * s).astype(np.float32),
        "d_words": packed_dT[0],
        "d_scales": packed_dT[1],
        "offs": striped(np.random.permutation(T)[:S]),
        "n1": striped(np.random.permutation(S)),
        "n2": striped(np.random.permutation(S)),
        "n3": striped(np.random.permutation(S)),
        "n4": striped(np.random.permutation(S)),
        "n5": striped8(np.stack([np.random.permutation(S) for _ in range(8)])),
        "n6": striped8(np.stack([np.random.permutation(S) for _ in range(8)])),
        "n7": striped8(np.stack([np.random.permutation(S) for _ in range(8)])),
        "cand": striped(np.random.permutation(T)[:C]),
        "k1": striped8(np.random.randint(0, G, (8, H))),
        "n8": striped8(np.stack([np.random.permutation(S) for _ in range(8)])),
        "n9": striped8(np.stack([np.random.permutation(S) for _ in range(8)])),
    }


def reference(x_words, x_scales, w1_words, w1_scales, gs, gk, d_words, d_scales, offs, n1, n2, n3, n4, n5, n6, n7, cand, k1, n8, n9):
    x_cand = unpack_weight(x_words, x_scales)[:, unstriped(cand)]
    xq = unpack_weight(x_words, x_scales)[:, unstriped(offs)]
    y = unpack_fp4(w1_words, w1_scales).T @ xq
    z = f64(gs) * (0.75 * (y[:, unstriped(n1)] * y[:, unstriped(n2)] - (y[:, unstriped(n3)] * y[:, unstriped(n4)])))
    a = 0.0625 * ((x_cand.T @ mxq(z, 0, "e4m3")))
    d_k1 = unpack_weight(d_words, d_scales)[np.arange(K)[:, None], runs(k1, K)]
    z2 = f64(gk) * (y + y[np.arange(H)[:, None], runs(n5, H)] - (np.maximum(y[np.arange(H)[:, None], runs(n6, H)], y[np.arange(H)[:, None], runs(n7, H)])))
    b = 0.0625 * ((d_k1.T @ mxq(z2, 0, "e4m3")))
    out_0 = (a - (a[np.arange(C)[:, None], runs(n8, C)])) / (np.abs(b) + np.abs(b[np.arange(H)[:, None], runs(n9, H)]) + 0.5)
    return (out_0,) + planes(out_0)

@@ -1,0 +1,259 @@
+from contextlib import ExitStack
+
+import concourse.mybir as mybir
+
+F32 = mybir.dt.float32
+BF16 = mybir.dt.bfloat16
+I32 = mybir.dt.int32
+U32 = mybir.dt.uint32
+U16 = mybir.dt.uint16
+U8 = mybir.dt.uint8
+FP8X4 = mybir.dt.float8_e4m3fn_x4
+FP4X4 = mybir.dt.float4_e2m1fn_x4
+ALU = mybir.AluOpType
+ACT = mybir.ActivationFunctionType
+
+P = 128
+PACK = 4
+S = 512
+T = 1024
+G = 2048
+HALF = S // 2
+SPARE = 16
+FLOPS = 3 * 2 * 512 * 512 * 512
+
+
+def tile_picked_cdkeynormbdettrim_none_po_kernel(
+    tc, x_words, x_scales, w1_words, w1_scales, gs, gk, d_words, d_scales,
+    offs, n1, n2, n3, n4, n5, n6, n7, cand, k1, n8, n9, out_0, out_1, out_2,
+):
+    nc = tc.nc
+    with ExitStack() as ctx:
+        pool = ctx.enter_context(tc.tile_pool(name="keep", bufs=1))
+        psum = ctx.enter_context(tc.psum_pool(name="psum", bufs=1))
+
+        def sb(name, shape, dtype):
+            return pool.tile(shape, dtype, name=name, align_bytes=64)
+
+        def load_list(name, dram):
+            tile = sb(name, [P, S // 16], U16)
+            nc.sync.dma_start(tile[:], dram)
+            return tile
+
+        def load_scale_rows(queues, tile, dram, first_partitions):
+            rows = dram[0].bitcast(I32)
+            for r, part in enumerate(first_partitions):
+                queues[r].dma_start(tile[part:P:32, :].bitcast(I32), rows[r:16:PACK, :])
+
+        def half_list(tile, h):
+            return tile[:, h * (HALF // 16) : (h + 1) * (HALF // 16)]
+
+        def cols(h):
+            return slice(h * HALF, (h + 1) * HALF)
+
+        def woven(tile):
+            return tile.rearrange("p (c i) t -> p c t i", i=4)
+
+        def by_rows(tile):
+            return tile.rearrange("p t (c i) -> p c t i", i=4)
+
+        xw = sb("xw", [P, T], I32)
+        xs = sb("xs", [P, T], U8)
+        ww = sb("ww", [P, 2 * S], U8)
+        ws = sb("ws", [P, S], U8)
+        dw = sb("dw", [P, G], I32)
+        ds = sb("ds", [P, G], U8)
+        key_scales = sb("key_scales", [P, S], U8)
+        y = [sb(f"y{t}", [P, 2 * S], F32) for t in range(PACK)]
+        ys = [sb(f"ys{t}", [P, S + SPARE], F32) for t in range(PACK)]
+
+        nc.vector.memset(ws[:].bitcast(I32), 0)
+        nc.vector.memset(xs[:].bitcast(I32), 0)
+        nc.vector.memset(ds[:].bitcast(I32), 0)
+        nc.vector.memset(key_scales[:].bitcast(I32), 0)
+        for t in range(PACK):
+            nc.vector.memset(y[t][:, S:], 0.0)
+        for t in range(PACK):
+            nc.vector.memset(ys[t][:, S:], 0.0)
+
+        offs_l = load_list("offs_l", offs)
+        nc.scalar.dma_start(ww[:].bitcast(I32), w1_words[0].bitcast(I32))
+        nc.sync.dma_start(xw[:], x_words[0].rearrange("p c r -> p (c r)").bitcast(I32))
+        load_scale_rows([nc.scalar] * 4, ws, w1_scales, (0, 1, 2, 3))
+        load_scale_rows([nc.sync] * 3 + [nc.gpsimd], xs, x_scales, (0, 1, 2, 3))
+        cand_l = load_list("cand_l", cand)
+        n6_l = load_list("n6_l", n6)
+        n7_l = load_list("n7_l", n7)
+        k1_l = load_list("k1_l", k1)
+        nc.sync.dma_start(dw[:], d_words[0].rearrange("p c r -> p (c r)").bitcast(I32))
+        load_scale_rows([nc.sync] * 4, ds, d_scales, (0, 1, 16, 17))
+        n5_l = load_list("n5_l", n5)
+        gk_sb = sb("gk_sb", [P, PACK], F32)
+        nc.sync.dma_start(gk_sb[:], gk.rearrange("(p t) o -> p (t o)", t=PACK))
+        gs_sb = sb("gs_sb", [P, PACK], F32)
+        nc.sync.dma_start(gs_sb[:], gs.rearrange("(p t) o -> p (t o)", t=PACK))
+        n1_l = load_list("n1_l", n1)
+        n3_l = load_list("n3_l", n3)
+        n2_l = load_list("n2_l", n2)
+        n4_l = load_list("n4_l", n4)
+        n9_l = load_list("n9_l", n9)
+        n8_l = load_list("n8_l", n8)
+
+        gs34 = sb("gs34", [P, PACK], F32)
+        nc.gpsimd.tensor_scalar(gs34[:], gs_sb[:], 0.75, 0.0, ALU.mult, ALU.add)
+
+        def gather_packed(name, words, scales, offsets):
+            gw = sb(name + "_gw", [P, S], U32)
+            nc.vector.tensor_copy(gw[:], words[:].bitcast(U32).indirect(offsets[:]))
+            gb = sb(name + "_gb", [P, S], U8)
+            nc.vector.tensor_copy(gb[:], scales[:].indirect(offsets[:]))
+            return gw, gb
+
+        def deal(name, src, dtype):
+            dst = sb(name, [P, S], dtype)
+            nc.vector.tensor_copy(
+                dst[:].rearrange("p (t m) -> p m t", t=PACK),
+                src[:].bitcast(dtype).rearrange("p (m t) -> p m t", t=PACK),
+            )
+            return dst
+
+        w_words = sb("w_words", [P, 2 * S], U8)
+        nc.vector.tensor_copy(
+            w_words[:].rearrange("p (t m b) -> p m t b", t=PACK, b=2),
+            ww[:].rearrange("p (m t b) -> p m t b", t=PACK, b=2),
+        )
+        w_scales = deal("w_scales", ws, U8)
+        xq_words, xq_scales = gather_packed("xq", xw, xs, offs_l)
+
+        y_ps = [psum.tile([P, S], F32, name=f"y_ps{t}", tag=f"bank{t}") for t in range(PACK)]
+        for t in range(PACK):
+            nc.tensor.matmul_mx(
+                y_ps[t][:],
+                lhsT=w_words[:, 2 * P * t : 2 * P * (t + 1)].bitcast(FP4X4),
+                lhsT_scale=w_scales[:, P * t : P * (t + 1)],
+                rhs=xq_words[:].bitcast(FP8X4),
+                rhs_scale=xq_scales[:],
+                start=True, stop=True,
+            )
+
+        g6 = [sb(f"g6_{t}", [P, S], F32) for t in range(PACK)]
+        g7 = [sb(f"g7_{t}", [P, S], F32) for t in range(PACK)]
+        for t in range(PACK):
+            nc.scalar.copy(y[t][:, :S], y_ps[t][:])
+            nc.scalar.activation(g6[t][:], y[t][:].indirect(n6_l[:]), ACT.Copy)
+            nc.scalar.activation(g7[t][:], y[t][:].indirect(n7_l[:]), ACT.Copy)
+
+        cand_gw, cand_gb = gather_packed("cand", xw, xs, cand_l)
+        key_gw, key_gb = gather_packed("key", dw, ds, k1_l)
+        key_dealt = deal("key_dealt", key_gb, U8)
+        for r, part in enumerate((0, 1, 16, 17)):
+            nc.sync.dma_start(key_scales[r:P:32, :].bitcast(I32), key_dealt[part:P:32, :].bitcast(I32))
+        key_words = deal("key_words", key_gw, I32)
+        cand_words = deal("cand_words", cand_gw, I32)
+        cand_scales = deal("cand_scales", cand_gb, U8)
+
+        larger = [sb(f"larger{t}", [P, S], F32) for t in range(PACK)]
+        diff = [sb(f"diff{t}", [P, S], F32) for t in range(PACK)]
+        z2_f32 = sb("z2_f32", [P, PACK, S], F32)
+        for t in range(PACK + 1):
+            if t < PACK:
+                nc.vector.tensor_tensor(larger[t][:], g6[t][:], g7[t][:], ALU.max)
+            if t > 0:
+                nc.vector.tensor_tensor(z2_f32[:, t - 1, :], diff[t - 1][:], y[t - 1][:, :S], ALU.add)
+            if t < PACK:
+                nc.vector.tensor_tensor(diff[t][:], y[t][:].indirect(n5_l[:]), larger[t][:], ALU.subtract)
+
+        def quantized(name):
+            return sb(name + "_bf", [P, S, PACK], BF16), sb(name + "_codes", [P, S], U32), sb(name + "_scales", [P, S], U8)
+
+        def quantize(tiles, h):
+            bf, codes, scales = tiles
+            nc.vector.quantize_mx(
+                codes[:, cols(h)].bitcast(FP8X4), scales[:, cols(h)],
+                bf[:, cols(h), :].rearrange("p c t -> p (c t)"),
+            )
+
+        z2_q = quantized("z2")
+        gk_wide = gk_sb[:].unsqueeze(1).unsqueeze(3).to_broadcast([P, HALF // 4, PACK, 4])
+        for h in range(2):
+            nc.vector.tensor_tensor(woven(z2_q[0][:, cols(h), :]), by_rows(z2_f32[:, :, cols(h)]), gk_wide, ALU.mult)
+        for h in range(2):
+            quantize(z2_q, h)
+
+        b_ps = [psum.tile([P, S], F32, name=f"b_ps{t}", tag=f"bank{PACK + t}") for t in range(PACK)]
+        for t in range(PACK):
+            nc.tensor.matmul_mx(
+                b_ps[t][:],
+                lhsT=key_words[:, P * t : P * (t + 1)].bitcast(FP8X4),
+                lhsT_scale=key_scales[:, P * t : P * (t + 1)],
+                rhs=z2_q[1][:].bitcast(FP8X4),
+                rhs_scale=z2_q[2][:],
+                start=True, stop=True,
+            )
+
+        g1 = [sb(f"g1_{t}", [P, S], F32) for t in range(PACK)]
+        g3 = [sb(f"g3_{t}", [P, S], F32) for t in range(PACK)]
+        prod12 = sb("prod12", [P, PACK, S], F32)
+        prod34 = sb("prod34", [P, PACK, S], F32)
+        for t in range(PACK):
+            nc.scalar.activation(ys[t][:, :S], y_ps[t][:], ACT.Copy, scale=gs34[:, t : t + 1])
+            nc.scalar.activation(g1[t][:], ys[t][:].indirect(n1_l[:]), ACT.Copy)
+            nc.scalar.activation(g3[t][:], ys[t][:].indirect(n3_l[:]), ACT.Copy)
+            nc.vector.tensor_tensor(prod12[:, t, :], y[t][:].indirect(n2_l[:]), g1[t][:], ALU.mult)
+            nc.vector.tensor_tensor(prod34[:, t, :], y[t][:].indirect(n4_l[:]), g3[t][:], ALU.mult)
+        z_q = quantized("z")
+        for h in range(2):
+            nc.vector.tensor_tensor(
+                woven(z_q[0][:, cols(h), :]), by_rows(prod12[:, :, cols(h)]), by_rows(prod34[:, :, cols(h)]), ALU.subtract
+            )
+        for h in range(2):
+            quantize(z_q, h)
+
+        a_ps = [psum.tile([P, S], F32, name=f"a_ps{t}", tag=f"bank{t}") for t in range(PACK)]
+        for h in range(2):
+            for t in range(PACK):
+                nc.tensor.matmul_mx(
+                    a_ps[t][:, cols(h)],
+                    lhsT=cand_words[:, P * t : P * (t + 1)].bitcast(FP8X4),
+                    lhsT_scale=cand_scales[:, P * t : P * (t + 1)],
+                    rhs=z_q[1][:, cols(h)].bitcast(FP8X4),
+                    rhs_scale=z_q[2][:, cols(h)],
+                    start=True, stop=True,
+                )
+
+        size = [sb(f"size{t}", [P, S], F32) for t in range(PACK)]
+        g9 = [sb(f"g9_{t}", [P, S], F32) for t in range(PACK)]
+        den = [sb(f"den{t}", [P, S], F32) for t in range(PACK)]
+        root = [sb(f"root{t}", [P, S], F32) for t in range(PACK)]
+        inv = [sb(f"inv{t}", [P, S], F32) for t in range(PACK)]
+        for t in range(PACK):
+            nc.scalar.activation(size[t][:], b_ps[t][:], ACT.Abs, scale=0.0625)
+            for h in range(2):
+                nc.scalar.activation(g9[t][:, cols(h)], size[t][:].indirect(half_list(n9_l, h)), ACT.Copy)
+            nc.vector.scalar_tensor_tensor(den[t][:], size[t][:], 0.5, g9[t][:], ALU.add, ALU.add)
+        for t in range(PACK):
+            nc.scalar.activation(root[t][:], den[t][:], ACT.Abs_reciprocal_sqrt)
+            nc.vector.tensor_tensor(inv[t][:], root[t][:], root[t][:], ALU.mult)
+
+        a = [sb(f"a{t}", [P, S], F32) for t in range(PACK)]
+        g8 = [sb(f"g8_{t}", [P, S], F32) for t in range(PACK)]
+        num = [sb(f"num{t}", [P, S], F32) for t in range(PACK)]
+        res = [sb(f"res{h}", [P, PACK, HALF], F32) for h in range(2)]
+        out_q = quantized("out")
+        out_rows = out_0.rearrange("(p t) j -> p t j", t=PACK)
+        out_words = out_1[0].rearrange("p c r -> p (c r)").bitcast(I32)
+        for h in range(2):
+            for t in range(PACK):
+                if h == 0:
+                    nc.scalar.activation(a[t][:], a_ps[t][:], ACT.Copy, scale=0.0625)
+                nc.scalar.activation(g8[t][:, cols(h)], a[t][:].indirect(half_list(n8_l, h)), ACT.Copy)
+                nc.vector.tensor_tensor(num[t][:, cols(h)], a[t][:, cols(h)], g8[t][:, cols(h)], ALU.subtract)
+                nc.vector.tensor_tensor(res[h][:, t, :], num[t][:, cols(h)], inv[t][:, cols(h)], ALU.mult)
+                nc.sync.dma_start(out_rows[:, t, cols(h)], res[h][:, t, :])
+            nc.vector.tensor_copy(woven(out_q[0][:, cols(h), :]), by_rows(res[h][:]))
+            quantize(out_q, h)
+            nc.sync.dma_start(out_words[:, cols(h)], out_q[1][:, cols(h)].bitcast(I32))
+        out_scale_rows = out_2[0].bitcast(I32)
+        for q in range(4):
+            queue = nc.sync if q % 2 == 0 else nc.scalar
+            queue.dma_start(out_scale_rows[4 * q : 4 * q + 4, :], out_q[2][32 * q : 32 * q + 4, :].bitcast(I32))

@@ -1,6 +1,7 @@
 from contextlib import ExitStack
 
 import concourse.mybir as mybir
+from concourse.masks import make_identity
 
 F32 = mybir.dt.float32
 BF16 = mybir.dt.bfloat16
@@ -20,6 +21,12 @@ T = 1024
 G = 2048
 HALF = S // 2
 SPARE = 16
+N4_ON_SCALAR = 1
+EARLY_ROOT = 2
+WEAVE0_ON_SCALAR = 1
+YS_ON_VECTOR = 4
+SQ_ON_SCALAR = 0
+A_ON_VECTOR = 1
 FLOPS = 3 * 2 * 512 * 512 * 512
 
 
@@ -40,10 +47,13 @@ def tile_picked_cdkeynormbdettrim_none_po_kernel(
             nc.sync.dma_start(tile[:], dram)
             return tile
 
-        def load_scale_rows(queues, tile, dram, first_partitions):
+        def load_scale_rows(queues, tile, dram):
             rows = dram[0].bitcast(I32)
-            for r, part in enumerate(first_partitions):
-                queues[r].dma_start(tile[part:P:32, :].bitcast(I32), rows[r:16:PACK, :])
+            for q, queue in enumerate(queues):
+                four = rows[4 * q : 4 * q + 4, :]
+                queue.dma_start(
+                    tile[32 * q : 32 * (q + 1), :].bitcast(I32), four.unsqueeze(0).to_broadcast([8, 4, four.shape[1]])
+                )
 
         def half_list(tile, h):
             return tile[:, h * (HALF // 16) : (h + 1) * (HALF // 16)]
@@ -67,9 +77,8 @@ def tile_picked_cdkeynormbdettrim_none_po_kernel(
         y = [sb(f"y{t}", [P, 2 * S], F32) for t in range(PACK)]
         ys = [sb(f"ys{t}", [P, S + SPARE], F32) for t in range(PACK)]
 
-        nc.vector.memset(ws[:].bitcast(I32), 0)
-        nc.vector.memset(xs[:].bitcast(I32), 0)
-        nc.vector.memset(ds[:].bitcast(I32), 0)
+        warm = sb("warm", [P, 2], F32)
+        nc.vector.memset(warm[:, 0:1], 1.0)
         nc.vector.memset(key_scales[:].bitcast(I32), 0)
         for t in range(PACK):
             nc.vector.memset(y[t][:, S:], 0.0)
@@ -77,16 +86,17 @@ def tile_picked_cdkeynormbdettrim_none_po_kernel(
             nc.vector.memset(ys[t][:, S:], 0.0)
 
         offs_l = load_list("offs_l", offs)
-        nc.scalar.dma_start(ww[:].bitcast(I32), w1_words[0].bitcast(I32))
+        nc.sync.dma_start(ww[:].bitcast(I32), w1_words[0].bitcast(I32))
+        load_scale_rows([nc.sync] * 4, xs, x_scales)
         nc.sync.dma_start(xw[:], x_words[0].rearrange("p c r -> p (c r)").bitcast(I32))
-        load_scale_rows([nc.scalar] * 4, ws, w1_scales, (0, 1, 2, 3))
-        load_scale_rows([nc.sync] * 3 + [nc.gpsimd], xs, x_scales, (0, 1, 2, 3))
+        load_scale_rows([nc.sync] * 4, ws, w1_scales)
+        nc.scalar.activation(warm[:, 1:2], warm[:, 0:1], ACT.Abs_reciprocal_sqrt)
         cand_l = load_list("cand_l", cand)
         n6_l = load_list("n6_l", n6)
         n7_l = load_list("n7_l", n7)
-        k1_l = load_list("k1_l", k1)
         nc.sync.dma_start(dw[:], d_words[0].rearrange("p c r -> p (c r)").bitcast(I32))
-        load_scale_rows([nc.sync] * 4, ds, d_scales, (0, 1, 16, 17))
+        k1_l = load_list("k1_l", k1)
+        nc.sync.dma_start(ds[:].bitcast(I32), d_scales[0].bitcast(I32).unsqueeze(1).to_broadcast([16, 8, G // 4]))
         n5_l = load_list("n5_l", n5)
         gk_sb = sb("gk_sb", [P, PACK], F32)
         nc.sync.dma_start(gk_sb[:], gk.rearrange("(p t) o -> p (t o)", t=PACK))
@@ -99,15 +109,17 @@ def tile_picked_cdkeynormbdettrim_none_po_kernel(
         n9_l = load_list("n9_l", n9)
         n8_l = load_list("n8_l", n8)
 
+        ident = sb("ident", [P, P], F32)
+        make_identity(nc, ident[:])
+        half_col = sb("half_col", [P, 1], F32)
+        nc.vector.memset(half_col[:], 0.5)
         gs34 = sb("gs34", [P, PACK], F32)
         nc.gpsimd.tensor_scalar(gs34[:], gs_sb[:], 0.75, 0.0, ALU.mult, ALU.add)
 
-        def gather_packed(name, words, scales, offsets):
-            gw = sb(name + "_gw", [P, S], U32)
-            nc.vector.tensor_copy(gw[:], words[:].bitcast(U32).indirect(offsets[:]))
-            gb = sb(name + "_gb", [P, S], U8)
-            nc.vector.tensor_copy(gb[:], scales[:].indirect(offsets[:]))
-            return gw, gb
+        def gather(name, window, dtype, offsets):
+            picked = sb(name, [P, S], dtype)
+            nc.vector.tensor_copy(picked[:], window[:].bitcast(dtype).indirect(offsets[:]))
+            return picked
 
         def deal(name, src, dtype):
             dst = sb(name, [P, S], dtype)
@@ -119,11 +131,12 @@ def tile_picked_cdkeynormbdettrim_none_po_kernel(
 
         w_words = sb("w_words", [P, 2 * S], U8)
         nc.vector.tensor_copy(
-            w_words[:].rearrange("p (t m b) -> p m t b", t=PACK, b=2),
-            ww[:].rearrange("p (m t b) -> p m t b", t=PACK, b=2),
+            w_words[:].bitcast(U16).rearrange("p (t m) -> p m t", t=PACK),
+            ww[:].bitcast(U16).rearrange("p (m t) -> p m t", t=PACK),
         )
+        xq_scales = gather("xq_scales", xs, U8, offs_l)
+        xq_words = gather("xq_words", xw, U32, offs_l)
         w_scales = deal("w_scales", ws, U8)
-        xq_words, xq_scales = gather_packed("xq", xw, xs, offs_l)
 
         y_ps = [psum.tile([P, S], F32, name=f"y_ps{t}", tag=f"bank{t}") for t in range(PACK)]
         for t in range(PACK):
@@ -143,25 +156,30 @@ def tile_picked_cdkeynormbdettrim_none_po_kernel(
             nc.scalar.activation(g6[t][:], y[t][:].indirect(n6_l[:]), ACT.Copy)
             nc.scalar.activation(g7[t][:], y[t][:].indirect(n7_l[:]), ACT.Copy)
 
-        cand_gw, cand_gb = gather_packed("cand", xw, xs, cand_l)
-        key_gw, key_gb = gather_packed("key", dw, ds, k1_l)
+        cand_gw = gather("cand_gw", xw, U32, cand_l)
+        cand_gb = gather("cand_gb", xs, U8, cand_l)
+        key_gb = gather("key_gb", ds, U8, k1_l)
+        key_gw = gather("key_gw", dw, U32, k1_l)
         key_dealt = deal("key_dealt", key_gb, U8)
-        for r, part in enumerate((0, 1, 16, 17)):
-            nc.sync.dma_start(key_scales[r:P:32, :].bitcast(I32), key_dealt[part:P:32, :].bitcast(I32))
-        key_words = deal("key_words", key_gw, I32)
+        for r in range(PACK):
+            nc.sync.dma_start(key_scales[r:P:32, :].bitcast(I32), key_dealt[8 * r : P : 32, :].bitcast(I32))
         cand_words = deal("cand_words", cand_gw, I32)
         cand_scales = deal("cand_scales", cand_gb, U8)
+        key_words = deal("key_words", key_gw, I32)
 
-        larger = [sb(f"larger{t}", [P, S], F32) for t in range(PACK)]
+        size = [sb(f"size{t}", [P, 2 * S], F32) for t in range(PACK)]
+        larger = [size[t][:, S:] for t in range(PACK)]
         diff = [sb(f"diff{t}", [P, S], F32) for t in range(PACK)]
         z2_f32 = sb("z2_f32", [P, PACK, S], F32)
         for t in range(PACK + 1):
             if t < PACK:
-                nc.vector.tensor_tensor(larger[t][:], g6[t][:], g7[t][:], ALU.max)
+                nc.vector.tensor_tensor(larger[t], g6[t][:], g7[t][:], ALU.max)
+            if 0 < t <= YS_ON_VECTOR:
+                nc.vector.tensor_scalar(ys[t - 1][:, :S], y[t - 1][:, :S], gs34[:, t - 1 : t], None, ALU.mult)
             if t > 0:
                 nc.vector.tensor_tensor(z2_f32[:, t - 1, :], diff[t - 1][:], y[t - 1][:, :S], ALU.add)
             if t < PACK:
-                nc.vector.tensor_tensor(diff[t][:], y[t][:].indirect(n5_l[:]), larger[t][:], ALU.subtract)
+                nc.vector.tensor_tensor(diff[t][:], y[t][:].indirect(n5_l[:]), larger[t], ALU.subtract)
 
         def quantized(name):
             return sb(name + "_bf", [P, S, PACK], BF16), sb(name + "_codes", [P, S], U32), sb(name + "_scales", [P, S], U8)
@@ -196,11 +214,31 @@ def tile_picked_cdkeynormbdettrim_none_po_kernel(
         prod12 = sb("prod12", [P, PACK, S], F32)
         prod34 = sb("prod34", [P, PACK, S], F32)
         for t in range(PACK):
-            nc.scalar.activation(ys[t][:, :S], y_ps[t][:], ACT.Copy, scale=gs34[:, t : t + 1])
+            if t >= YS_ON_VECTOR:
+                nc.scalar.activation(ys[t][:, :S], y_ps[t][:], ACT.Copy, scale=gs34[:, t : t + 1])
             nc.scalar.activation(g1[t][:], ys[t][:].indirect(n1_l[:]), ACT.Copy)
             nc.scalar.activation(g3[t][:], ys[t][:].indirect(n3_l[:]), ACT.Copy)
             nc.vector.tensor_tensor(prod12[:, t, :], y[t][:].indirect(n2_l[:]), g1[t][:], ALU.mult)
-            nc.vector.tensor_tensor(prod34[:, t, :], y[t][:].indirect(n4_l[:]), g3[t][:], ALU.mult)
+            if t < PACK - N4_ON_SCALAR:
+                nc.vector.tensor_tensor(prod34[:, t, :], y[t][:].indirect(n4_l[:]), g3[t][:], ALU.mult)
+            else:
+                g4 = sb(f"g4_{t}", [P, S], F32)
+                nc.scalar.activation(g4[:], y[t][:].indirect(n4_l[:]), ACT.Copy)
+                nc.vector.tensor_tensor(prod34[:, t, :], g4[:], g3[t][:], ALU.mult)
+
+        g9 = [sb(f"g9_{t}", [P, S], F32) for t in range(PACK)]
+        root = [sb(f"root{t}", [P, S], F32) for t in range(PACK)]
+        inv = [sb(f"inv{t}", [P, S], F32) for t in range(PACK)]
+        den_ps = [psum.tile([P, S], F32, name=f"den_ps{jb}", tag=f"bank{jb}") for jb in range(PACK)]
+        for t in range(PACK):
+            nc.scalar.activation(size[t][:, :S], b_ps[t][:], ACT.Abs, scale=0.0625)
+            nc.scalar.activation(g9[t][:], size[t][:].indirect(n9_l[:]), ACT.Copy)
+            for jb in range(PACK):
+                for term, first in ((size[t], True), (g9[t], False)):
+                    nc.tensor.matmul(
+                        den_ps[jb][:, P * t : P * (t + 1)], lhsT=term[:, P * jb : P * (jb + 1)], rhs=ident[:],
+                        start=first, stop=not first, is_transpose=True,
+                    )
         z_q = quantized("z")
         for h in range(2):
             nc.vector.tensor_tensor(
@@ -209,9 +247,9 @@ def tile_picked_cdkeynormbdettrim_none_po_kernel(
         for h in range(2):
             quantize(z_q, h)
 
-        a_ps = [psum.tile([P, S], F32, name=f"a_ps{t}", tag=f"bank{t}") for t in range(PACK)]
-        for h in range(2):
-            for t in range(PACK):
+        a_ps = [psum.tile([P, S], F32, name=f"a_ps{t}", tag=f"bank{PACK + t}") for t in range(PACK)]
+        for t in range(PACK):
+            for h in range(2):
                 nc.tensor.matmul_mx(
                     a_ps[t][:, cols(h)],
                     lhsT=cand_words[:, P * t : P * (t + 1)].bitcast(FP8X4),
@@ -221,19 +259,26 @@ def tile_picked_cdkeynormbdettrim_none_po_kernel(
                     start=True, stop=True,
                 )
 
-        size = [sb(f"size{t}", [P, S], F32) for t in range(PACK)]
-        g9 = [sb(f"g9_{t}", [P, S], F32) for t in range(PACK)]
-        den = [sb(f"den{t}", [P, S], F32) for t in range(PACK)]
-        root = [sb(f"root{t}", [P, S], F32) for t in range(PACK)]
-        inv = [sb(f"inv{t}", [P, S], F32) for t in range(PACK)]
-        for t in range(PACK):
-            nc.scalar.activation(size[t][:], b_ps[t][:], ACT.Abs, scale=0.0625)
-            for h in range(2):
-                nc.scalar.activation(g9[t][:, cols(h)], size[t][:].indirect(half_list(n9_l, h)), ACT.Copy)
-            nc.vector.scalar_tensor_tensor(den[t][:], size[t][:], 0.5, g9[t][:], ALU.add, ALU.add)
-        for t in range(PACK):
-            nc.scalar.activation(root[t][:], den[t][:], ACT.Abs_reciprocal_sqrt)
-            nc.vector.tensor_tensor(inv[t][:], root[t][:], root[t][:], ALU.mult)
+        inv_ps = {}
+
+        def inverse(jb):
+            nc.scalar.activation(root[jb][:], den_ps[jb][:], ACT.Abs_reciprocal_sqrt, bias=half_col[:])
+            if jb < SQ_ON_SCALAR:
+                nc.scalar.activation(inv[jb][:], root[jb][:], ACT.Square)
+            else:
+                nc.vector.tensor_tensor(inv[jb][:], root[jb][:], root[jb][:], ALU.mult)
+            if jb % 2 == 1:
+                h = jb // 2
+                for pair in range(2):
+                    inv_ps[h, pair] = psum.tile([P, 2, HALF], F32, name=f"inv_ps{h}{pair}", tag=f"bank{2 * h + pair}")
+                    for t in (2 * pair, 2 * pair + 1):
+                        for u in range(2):
+                            nc.tensor.transpose(
+                                inv_ps[h, pair][:, t % 2, P * u : P * (u + 1)], inv[2 * h + u][:, P * t : P * (t + 1)], ident[:]
+                            )
+
+        for jb in range(EARLY_ROOT):
+            inverse(jb)
 
         a = [sb(f"a{t}", [P, S], F32) for t in range(PACK)]
         g8 = [sb(f"g8_{t}", [P, S], F32) for t in range(PACK)]
@@ -242,17 +287,37 @@ def tile_picked_cdkeynormbdettrim_none_po_kernel(
         out_q = quantized("out")
         out_rows = out_0.rearrange("(p t) j -> p t j", t=PACK)
         out_words = out_1[0].rearrange("p c r -> p (c r)").bitcast(I32)
-        for h in range(2):
-            for t in range(PACK):
-                if h == 0:
-                    nc.scalar.activation(a[t][:], a_ps[t][:], ACT.Copy, scale=0.0625)
-                nc.scalar.activation(g8[t][:, cols(h)], a[t][:].indirect(half_list(n8_l, h)), ACT.Copy)
-                nc.vector.tensor_tensor(num[t][:, cols(h)], a[t][:, cols(h)], g8[t][:, cols(h)], ALU.subtract)
-                nc.vector.tensor_tensor(res[h][:, t, :], num[t][:, cols(h)], inv[t][:, cols(h)], ALU.mult)
-                nc.sync.dma_start(out_rows[:, t, cols(h)], res[h][:, t, :])
-            nc.vector.tensor_copy(woven(out_q[0][:, cols(h), :]), by_rows(res[h][:]))
+        for t in range(A_ON_VECTOR):
+            nc.vector.tensor_scalar(a[t][:], a_ps[t][:], 0.0625, None, ALU.mult)
+        steps = [(h, t) for h in range(2) for t in range(PACK)]
+
+        def finish_half(h):
             quantize(out_q, h)
             nc.sync.dma_start(out_words[:, cols(h)], out_q[1][:, cols(h)].bitcast(I32))
+
+        for i in range(len(steps) + 1):
+            if i < len(steps):
+                h, t = steps[i]
+                if h == 0 and t >= A_ON_VECTOR:
+                    nc.scalar.activation(a[t][:], a_ps[t][:], ACT.Copy, scale=0.0625)
+                nc.scalar.activation(g8[t][:, cols(h)], a[t][:].indirect(half_list(n8_l, h)), ACT.Copy)
+                if EARLY_ROOT + i < PACK:
+                    inverse(EARLY_ROOT + i)
+                nc.vector.tensor_tensor(num[t][:, cols(h)], a[t][:, cols(h)], g8[t][:, cols(h)], ALU.subtract)
+            if i == PACK + 2 and not WEAVE0_ON_SCALAR:
+                finish_half(0)
+            if i > 0:
+                h, t = steps[i - 1]
+                nc.vector.tensor_tensor(res[h][:, t, :], num[t][:, cols(h)], inv_ps[h, t // 2][:, t % 2, :], ALU.mult)
+                nc.sync.dma_start(out_rows[:, t, cols(h)], res[h][:, t, :])
+            if i == PACK + 1 and not WEAVE0_ON_SCALAR:
+                nc.vector.tensor_copy(woven(out_q[0][:, cols(0), :]), by_rows(res[0][:]))
+            if i == 2 * PACK - 1 and WEAVE0_ON_SCALAR:
+                nc.scalar.copy(woven(out_q[0][:, cols(0), :]), by_rows(res[0][:]))
+        if WEAVE0_ON_SCALAR:
+            finish_half(0)
+        nc.vector.tensor_copy(woven(out_q[0][:, cols(1), :]), by_rows(res[1][:]))
+        finish_half(1)
         out_scale_rows = out_2[0].bitcast(I32)
         for q in range(4):
             queue = nc.sync if q % 2 == 0 else nc.scalar

@@ -21,7 +21,11 @@ T = 1024
 G = 2048
 HALF = S // 2
 SPARE = 16
-N4_ON_SCALAR = 1
+N5_FROM = 3
+N5_TO = 4
+N5_TILES = range(N5_FROM, N5_TO)
+PAIRS_ON_SCALAR = 0
+N4_ON_SCALAR = 0
 EARLY_ROOT = 2
 WEAVE0_ON_SCALAR = 1
 YS_ON_VECTOR = 4
@@ -98,8 +102,6 @@ def tile_picked_cdkeynormbdettrim_none_po_kernel(
         k1_l = load_list("k1_l", k1)
         nc.sync.dma_start(ds[:].bitcast(I32), d_scales[0].bitcast(I32).unsqueeze(1).to_broadcast([16, 8, G // 4]))
         n5_l = load_list("n5_l", n5)
-        gk_sb = sb("gk_sb", [P, PACK], F32)
-        nc.sync.dma_start(gk_sb[:], gk.rearrange("(p t) o -> p (t o)", t=PACK))
         gs_sb = sb("gs_sb", [P, PACK], F32)
         nc.sync.dma_start(gs_sb[:], gs.rearrange("(p t) o -> p (t o)", t=PACK))
         n1_l = load_list("n1_l", n1)
@@ -108,6 +110,8 @@ def tile_picked_cdkeynormbdettrim_none_po_kernel(
         n4_l = load_list("n4_l", n4)
         n9_l = load_list("n9_l", n9)
         n8_l = load_list("n8_l", n8)
+        gk_row = sb("gk_row", [P, S], F32)
+        nc.sync.dma_start(gk_row[:], gk.rearrange("k o -> o k").to_broadcast([P, S]))
 
         ident = sb("ident", [P, P], F32)
         make_identity(nc, ident[:])
@@ -130,13 +134,18 @@ def tile_picked_cdkeynormbdettrim_none_po_kernel(
             return dst
 
         w_words = sb("w_words", [P, 2 * S], U8)
-        nc.vector.tensor_copy(
-            w_words[:].bitcast(U16).rearrange("p (t m) -> p m t", t=PACK),
-            ww[:].bitcast(U16).rearrange("p (m t) -> p m t", t=PACK),
-        )
+        w_scales = sb("w_scales", [P, S], U8)
+
+        def deal_tiles(dst, src, tiles):
+            nc.vector.tensor_copy(
+                dst.rearrange("p (t m) -> p m t", t=PACK)[:, :, tiles], src.rearrange("p (m t) -> p m t", t=PACK)[:, :, tiles]
+            )
+
+        deal_tiles(w_words[:].bitcast(U16), ww[:].bitcast(U16), slice(0, PACK))
         xq_scales = gather("xq_scales", xs, U8, offs_l)
         xq_words = gather("xq_words", xw, U32, offs_l)
-        w_scales = deal("w_scales", ws, U8)
+        deal_tiles(w_scales[:], ws[:], slice(0, 1))
+        deal_tiles(w_scales[:], ws[:], slice(1, PACK))
 
         y_ps = [psum.tile([P, S], F32, name=f"y_ps{t}", tag=f"bank{t}") for t in range(PACK)]
         for t in range(PACK):
@@ -150,11 +159,15 @@ def tile_picked_cdkeynormbdettrim_none_po_kernel(
             )
 
         g6 = [sb(f"g6_{t}", [P, S], F32) for t in range(PACK)]
+        diff = [sb(f"diff{t}", [P, S], F32) for t in range(PACK)]
         g7 = [sb(f"g7_{t}", [P, S], F32) for t in range(PACK)]
         for t in range(PACK):
             nc.scalar.copy(y[t][:, :S], y_ps[t][:])
-            nc.scalar.activation(g6[t][:], y[t][:].indirect(n6_l[:]), ACT.Copy)
-            nc.scalar.activation(g7[t][:], y[t][:].indirect(n7_l[:]), ACT.Copy)
+            sign = -1.0 if t in N5_TILES else 1.0
+            nc.scalar.activation(g6[t][:], y[t][:].indirect(n6_l[:]), ACT.Copy, scale=sign)
+            nc.scalar.activation(g7[t][:], y[t][:].indirect(n7_l[:]), ACT.Copy, scale=sign)
+            if t in N5_TILES:
+                nc.scalar.activation(diff[t][:], y[t][:].indirect(n5_l[:]), ACT.Copy)
 
         cand_gw = gather("cand_gw", xw, U32, cand_l)
         cand_gb = gather("cand_gb", xs, U8, cand_l)
@@ -169,17 +182,26 @@ def tile_picked_cdkeynormbdettrim_none_po_kernel(
 
         size = [sb(f"size{t}", [P, 2 * S], F32) for t in range(PACK)]
         larger = [size[t][:, S:] for t in range(PACK)]
-        diff = [sb(f"diff{t}", [P, S], F32) for t in range(PACK)]
-        z2_f32 = sb("z2_f32", [P, PACK, S], F32)
+        sum_ps = [psum.tile([P, S], F32, name=f"sum_ps{jb}", tag=f"bank{PACK + jb}") for jb in range(PACK)]
+
+        def add_turned(banks, t, *terms):
+            for jb in range(PACK):
+                for i, term in enumerate(terms):
+                    nc.tensor.matmul(
+                        banks[jb][:, P * t : P * (t + 1)], lhsT=term[:, P * jb : P * (jb + 1)], rhs=ident[:],
+                        start=i == 0, stop=i == len(terms) - 1, is_transpose=True,
+                    )
+
         for t in range(PACK + 1):
             if t < PACK:
-                nc.vector.tensor_tensor(larger[t], g6[t][:], g7[t][:], ALU.max)
+                nc.vector.tensor_tensor(larger[t], g6[t][:], g7[t][:], ALU.min if t in N5_TILES else ALU.max)
             if 0 < t <= YS_ON_VECTOR:
                 nc.vector.tensor_scalar(ys[t - 1][:, :S], y[t - 1][:, :S], gs34[:, t - 1 : t], None, ALU.mult)
-            if t > 0:
-                nc.vector.tensor_tensor(z2_f32[:, t - 1, :], diff[t - 1][:], y[t - 1][:, :S], ALU.add)
-            if t < PACK:
+            if t in N5_TILES:
+                add_turned(sum_ps, t, y[t], diff[t], larger[t])
+            elif t < PACK:
                 nc.vector.tensor_tensor(diff[t][:], y[t][:].indirect(n5_l[:]), larger[t], ALU.subtract)
+                add_turned(sum_ps, t, y[t], diff[t])
 
         def quantized(name):
             return sb(name + "_bf", [P, S, PACK], BF16), sb(name + "_codes", [P, S], U32), sb(name + "_scales", [P, S], U8)
@@ -192,9 +214,24 @@ def tile_picked_cdkeynormbdettrim_none_po_kernel(
             )
 
         z2_q = quantized("z2")
-        gk_wide = gk_sb[:].unsqueeze(1).unsqueeze(3).to_broadcast([P, HALF // 4, PACK, 4])
+        z2_turned = [sb(f"z2_turned{jb}", [P, 2, P, 2], BF16) for jb in range(PACK)]
+        pairs_ps = [psum.tile([P, 2, 2, P], F32, name=f"pairs_ps{h}", tag=f"bank{h}") for h in range(2)]
+        for jb in range(PACK):
+            nc.vector.tensor_tensor(
+                z2_turned[jb][:],
+                sum_ps[jb][:].rearrange("j (u e p) -> j u p e", u=2, e=2),
+                gk_row[:].rearrange("j (p u e) -> j u p e", u=2, e=2),
+                ALU.mult,
+            )
+            words = z2_turned[jb][:].rearrange("j u p e -> j (u p e)").bitcast(F32)
+            for u in range(2):
+                nc.tensor.transpose(pairs_ps[jb // 2][:, jb % 2, u, :], words[:, P * u : P * (u + 1)], ident[:])
         for h in range(2):
-            nc.vector.tensor_tensor(woven(z2_q[0][:, cols(h), :]), by_rows(z2_f32[:, :, cols(h)]), gk_wide, ALU.mult)
+            z2_pairs = z2_q[0][:, cols(h), :].rearrange("p c t -> p (c t)").bitcast(F32).rearrange("p (b j u) -> p b j u", b=2, u=2)
+            if h < PAIRS_ON_SCALAR:
+                nc.scalar.copy(z2_pairs, pairs_ps[h][:].rearrange("p b u j -> p b j u"))
+            else:
+                nc.vector.tensor_copy(z2_pairs, pairs_ps[h][:].rearrange("p b u j -> p b j u"))
         for h in range(2):
             quantize(z2_q, h)
 
@@ -233,12 +270,7 @@ def tile_picked_cdkeynormbdettrim_none_po_kernel(
         for t in range(PACK):
             nc.scalar.activation(size[t][:, :S], b_ps[t][:], ACT.Abs, scale=0.0625)
             nc.scalar.activation(g9[t][:], size[t][:].indirect(n9_l[:]), ACT.Copy)
-            for jb in range(PACK):
-                for term, first in ((size[t], True), (g9[t], False)):
-                    nc.tensor.matmul(
-                        den_ps[jb][:, P * t : P * (t + 1)], lhsT=term[:, P * jb : P * (jb + 1)], rhs=ident[:],
-                        start=first, stop=not first, is_transpose=True,
-                    )
+            add_turned(den_ps, t, size[t], g9[t])
         z_q = quantized("z")
         for h in range(2):
             nc.vector.tensor_tensor(
@@ -309,7 +341,8 @@ def tile_picked_cdkeynormbdettrim_none_po_kernel(
             if i > 0:
                 h, t = steps[i - 1]
                 nc.vector.tensor_tensor(res[h][:, t, :], num[t][:, cols(h)], inv_ps[h, t // 2][:, t % 2, :], ALU.mult)
-                nc.sync.dma_start(out_rows[:, t, cols(h)], res[h][:, t, :])
+                if t % 2 == 1:
+                    nc.sync.dma_start(out_rows[:, t - 1 : t + 1, cols(h)], res[h][:, t - 1 : t + 1, :])
             if i == PACK + 1 and not WEAVE0_ON_SCALAR:
                 nc.vector.tensor_copy(woven(out_q[0][:, cols(0), :]), by_rows(res[0][:]))
             if i == 2 * PACK - 1 and WEAVE0_ON_SCALAR:

@@ -20,18 +20,17 @@ S = 512
 T = 1024
 G = 2048
 HALF = S // 2
+GROUP = 16
+QUAD = 32
+BLOCK_PARTS = 8
 SPARE = 16
-N5_FROM = 3
-N5_TO = 4
-N5_TILES = range(N5_FROM, N5_TO)
-PAIRS_ON_SCALAR = 0
-N4_ON_SCALAR = 0
-EARLY_ROOT = 2
-WEAVE0_ON_SCALAR = 1
-YS_ON_VECTOR = 4
-SQ_ON_SCALAR = 0
-A_ON_VECTOR = 1
-FLOPS = 3 * 2 * 512 * 512 * 512
+SCORE_SCALE = 0.0625
+
+N5_SCALAR_TILE = 3
+SQUARES_ON_SCALAR = 1
+A_TILES_ON_VECTOR = 3
+
+FLOPS = 3 * 2 * S * S * S
 
 
 def tile_picked_cdkeynormbdettrim_none_po_kernel(
@@ -46,24 +45,34 @@ def tile_picked_cdkeynormbdettrim_none_po_kernel(
         def sb(name, shape, dtype):
             return pool.tile(shape, dtype, name=name, align_bytes=64)
 
+        def sb_rows(name, width):
+            return [sb(f"{name}{t}", [P, width], F32) for t in range(PACK)]
+
+        def banks(name, first):
+            return [psum.tile([P, S], F32, name=f"{name}{t}", tag=f"bank{first + t}") for t in range(PACK)]
+
         def load_list(name, dram):
-            tile = sb(name, [P, S // 16], U16)
+            tile = sb(name, [P, S // GROUP], U16)
             nc.sync.dma_start(tile[:], dram)
             return tile
 
-        def load_scale_rows(queues, tile, dram):
-            rows = dram[0].bitcast(I32)
-            for q, queue in enumerate(queues):
-                four = rows[4 * q : 4 * q + 4, :]
-                queue.dma_start(
-                    tile[32 * q : 32 * (q + 1), :].bitcast(I32), four.unsqueeze(0).to_broadcast([8, 4, four.shape[1]])
-                )
+        def load_words(tile, dram):
+            nc.sync.dma_start(tile[:], dram[0].rearrange("p c r -> p (c r)").bitcast(I32))
 
-        def half_list(tile, h):
-            return tile[:, h * (HALF // 16) : (h + 1) * (HALF // 16)]
+        def load_quadrant_scales(tile, dram):
+            rows = dram[0].bitcast(I32)
+            for q in range(P // QUAD):
+                four = rows[PACK * q : PACK * (q + 1), :]
+                nc.sync.dma_start(
+                    tile[QUAD * q : QUAD * (q + 1), :].bitcast(I32),
+                    four.unsqueeze(0).to_broadcast([QUAD // PACK, PACK, four.shape[1]]),
+                )
 
         def cols(h):
             return slice(h * HALF, (h + 1) * HALF)
+
+        def block(i):
+            return slice(P * i, P * (i + 1))
 
         def woven(tile):
             return tile.rearrange("p (c i) t -> p c t i", i=4)
@@ -71,15 +80,15 @@ def tile_picked_cdkeynormbdettrim_none_po_kernel(
         def by_rows(tile):
             return tile.rearrange("p t (c i) -> p c t i", i=4)
 
-        xw = sb("xw", [P, T], I32)
-        xs = sb("xs", [P, T], U8)
-        ww = sb("ww", [P, 2 * S], U8)
-        ws = sb("ws", [P, S], U8)
-        dw = sb("dw", [P, G], I32)
-        ds = sb("ds", [P, G], U8)
+        x_w = sb("x_w", [P, T], I32)
+        x_s = sb("x_s", [P, T], U8)
+        w1_w = sb("w1_w", [P, 2 * S], U8)
+        w1_s = sb("w1_s", [P, S], U8)
+        d_w = sb("d_w", [P, G], I32)
+        d_s = sb("d_s", [P, G], U8)
         key_scales = sb("key_scales", [P, S], U8)
-        y = [sb(f"y{t}", [P, 2 * S], F32) for t in range(PACK)]
-        ys = [sb(f"ys{t}", [P, S + SPARE], F32) for t in range(PACK)]
+        y = sb_rows("y", 2 * S)
+        y_gs = sb_rows("y_gs", S + SPARE)
 
         warm = sb("warm", [P, 2], F32)
         nc.vector.memset(warm[:, 0:1], 1.0)
@@ -87,23 +96,26 @@ def tile_picked_cdkeynormbdettrim_none_po_kernel(
         for t in range(PACK):
             nc.vector.memset(y[t][:, S:], 0.0)
         for t in range(PACK):
-            nc.vector.memset(ys[t][:, S:], 0.0)
+            nc.vector.memset(y_gs[t][:, S:], 0.0)
 
         offs_l = load_list("offs_l", offs)
-        nc.sync.dma_start(ww[:].bitcast(I32), w1_words[0].bitcast(I32))
-        load_scale_rows([nc.sync] * 4, xs, x_scales)
-        nc.sync.dma_start(xw[:], x_words[0].rearrange("p c r -> p (c r)").bitcast(I32))
-        load_scale_rows([nc.sync] * 4, ws, w1_scales)
+        nc.sync.dma_start(w1_w[:].bitcast(I32), w1_words[0].bitcast(I32))
+        load_quadrant_scales(x_s, x_scales)
+        load_words(x_w, x_words)
+        load_quadrant_scales(w1_s, w1_scales)
         nc.scalar.activation(warm[:, 1:2], warm[:, 0:1], ACT.Abs_reciprocal_sqrt)
         cand_l = load_list("cand_l", cand)
         n6_l = load_list("n6_l", n6)
         n7_l = load_list("n7_l", n7)
-        nc.sync.dma_start(dw[:], d_words[0].rearrange("p c r -> p (c r)").bitcast(I32))
+        load_words(d_w, d_words)
         k1_l = load_list("k1_l", k1)
-        nc.sync.dma_start(ds[:].bitcast(I32), d_scales[0].bitcast(I32).unsqueeze(1).to_broadcast([16, 8, G // 4]))
+        nc.sync.dma_start(
+            d_s[:].bitcast(I32),
+            d_scales[0].bitcast(I32).unsqueeze(1).to_broadcast([P // BLOCK_PARTS, BLOCK_PARTS, G // 4]),
+        )
         n5_l = load_list("n5_l", n5)
-        gs_sb = sb("gs_sb", [P, PACK], F32)
-        nc.sync.dma_start(gs_sb[:], gs.rearrange("(p t) o -> p (t o)", t=PACK))
+        gs_rows = sb("gs_rows", [P, PACK], F32)
+        nc.sync.dma_start(gs_rows[:], gs.rearrange("(p t) o -> p (t o)", t=PACK))
         n1_l = load_list("n1_l", n1)
         n3_l = load_list("n3_l", n3)
         n2_l = load_list("n2_l", n2)
@@ -115,243 +127,244 @@ def tile_picked_cdkeynormbdettrim_none_po_kernel(
 
         ident = sb("ident", [P, P], F32)
         make_identity(nc, ident[:])
-        half_col = sb("half_col", [P, 1], F32)
-        nc.vector.memset(half_col[:], 0.5)
-        gs34 = sb("gs34", [P, PACK], F32)
-        nc.gpsimd.tensor_scalar(gs34[:], gs_sb[:], 0.75, 0.0, ALU.mult, ALU.add)
+        one_half = sb("one_half", [P, 1], F32)
+        nc.vector.memset(one_half[:], 0.5)
+        z_factor = sb("z_factor", [P, PACK], F32)
+        nc.gpsimd.tensor_scalar(z_factor[:], gs_rows[:], 0.75, 0.0, ALU.mult, ALU.add)
 
-        def gather(name, window, dtype, offsets):
+        def gather_packed(name, window, dtype, offsets):
             picked = sb(name, [P, S], dtype)
             nc.vector.tensor_copy(picked[:], window[:].bitcast(dtype).indirect(offsets[:]))
             return picked
 
-        def deal(name, src, dtype):
-            dst = sb(name, [P, S], dtype)
+        def deal(dst, src, tiles=slice(0, PACK)):
             nc.vector.tensor_copy(
-                dst[:].rearrange("p (t m) -> p m t", t=PACK),
-                src[:].bitcast(dtype).rearrange("p (m t) -> p m t", t=PACK),
+                dst.rearrange("p (t m) -> p m t", t=PACK)[:, :, tiles],
+                src.rearrange("p (m t) -> p m t", t=PACK)[:, :, tiles],
             )
+
+        def dealt(name, src, dtype):
+            dst = sb(name, [P, S], dtype)
+            deal(dst[:], src[:].bitcast(dtype))
             return dst
+
+        def mx_product(out, words, words_dtype, scales, codes, code_scales):
+            nc.tensor.matmul_mx(
+                out, lhsT=words.bitcast(words_dtype), lhsT_scale=scales,
+                rhs=codes.bitcast(FP8X4), rhs_scale=code_scales, start=True, stop=True,
+            )
 
         w_words = sb("w_words", [P, 2 * S], U8)
         w_scales = sb("w_scales", [P, S], U8)
+        deal(w_words[:].bitcast(U16), w1_w[:].bitcast(U16))
+        xq_scales = gather_packed("xq_scales", x_s, U8, offs_l)
+        xq_words = gather_packed("xq_words", x_w, U32, offs_l)
+        deal(w_scales[:], w1_s[:], slice(0, 1))
+        deal(w_scales[:], w1_s[:], slice(1, PACK))
 
-        def deal_tiles(dst, src, tiles):
-            nc.vector.tensor_copy(
-                dst.rearrange("p (t m) -> p m t", t=PACK)[:, :, tiles], src.rearrange("p (m t) -> p m t", t=PACK)[:, :, tiles]
-            )
-
-        deal_tiles(w_words[:].bitcast(U16), ww[:].bitcast(U16), slice(0, PACK))
-        xq_scales = gather("xq_scales", xs, U8, offs_l)
-        xq_words = gather("xq_words", xw, U32, offs_l)
-        deal_tiles(w_scales[:], ws[:], slice(0, 1))
-        deal_tiles(w_scales[:], ws[:], slice(1, PACK))
-
-        y_ps = [psum.tile([P, S], F32, name=f"y_ps{t}", tag=f"bank{t}") for t in range(PACK)]
+        y_ps = banks("y_ps", 0)
         for t in range(PACK):
-            nc.tensor.matmul_mx(
-                y_ps[t][:],
-                lhsT=w_words[:, 2 * P * t : 2 * P * (t + 1)].bitcast(FP4X4),
-                lhsT_scale=w_scales[:, P * t : P * (t + 1)],
-                rhs=xq_words[:].bitcast(FP8X4),
-                rhs_scale=xq_scales[:],
-                start=True, stop=True,
+            mx_product(
+                y_ps[t][:], w_words[:, 2 * P * t : 2 * P * (t + 1)], FP4X4, w_scales[:, block(t)], xq_words[:], xq_scales[:]
             )
 
-        g6 = [sb(f"g6_{t}", [P, S], F32) for t in range(PACK)]
-        diff = [sb(f"diff{t}", [P, S], F32) for t in range(PACK)]
-        g7 = [sb(f"g7_{t}", [P, S], F32) for t in range(PACK)]
+        y_n6 = sb_rows("y_n6_", S)
+        z2_term = sb_rows("z2_term", S)
+        y_n7 = sb_rows("y_n7_", S)
         for t in range(PACK):
             nc.scalar.copy(y[t][:, :S], y_ps[t][:])
-            sign = -1.0 if t in N5_TILES else 1.0
-            nc.scalar.activation(g6[t][:], y[t][:].indirect(n6_l[:]), ACT.Copy, scale=sign)
-            nc.scalar.activation(g7[t][:], y[t][:].indirect(n7_l[:]), ACT.Copy, scale=sign)
-            if t in N5_TILES:
-                nc.scalar.activation(diff[t][:], y[t][:].indirect(n5_l[:]), ACT.Copy)
+            sign = -1.0 if t == N5_SCALAR_TILE else 1.0
+            nc.scalar.activation(y_n6[t][:], y[t][:].indirect(n6_l[:]), ACT.Copy, scale=sign)
+            nc.scalar.activation(y_n7[t][:], y[t][:].indirect(n7_l[:]), ACT.Copy, scale=sign)
+            if t == N5_SCALAR_TILE:
+                nc.scalar.activation(z2_term[t][:], y[t][:].indirect(n5_l[:]), ACT.Copy)
 
-        cand_gw = gather("cand_gw", xw, U32, cand_l)
-        cand_gb = gather("cand_gb", xs, U8, cand_l)
-        key_gb = gather("key_gb", ds, U8, k1_l)
-        key_gw = gather("key_gw", dw, U32, k1_l)
-        key_dealt = deal("key_dealt", key_gb, U8)
+        cand_picked_words = gather_packed("cand_picked_words", x_w, U32, cand_l)
+        cand_picked_scales = gather_packed("cand_picked_scales", x_s, U8, cand_l)
+        key_picked_scales = gather_packed("key_picked_scales", d_s, U8, k1_l)
+        key_picked_words = gather_packed("key_picked_words", d_w, U32, k1_l)
+        key_dealt_scales = dealt("key_dealt_scales", key_picked_scales, U8)
         for r in range(PACK):
-            nc.sync.dma_start(key_scales[r:P:32, :].bitcast(I32), key_dealt[8 * r : P : 32, :].bitcast(I32))
-        cand_words = deal("cand_words", cand_gw, I32)
-        cand_scales = deal("cand_scales", cand_gb, U8)
-        key_words = deal("key_words", key_gw, I32)
+            nc.sync.dma_start(
+                key_scales[r:P:QUAD, :].bitcast(I32), key_dealt_scales[BLOCK_PARTS * r : P : QUAD, :].bitcast(I32)
+            )
+        cand_words = dealt("cand_words", cand_picked_words, I32)
+        cand_scales = dealt("cand_scales", cand_picked_scales, U8)
+        key_words = dealt("key_words", key_picked_words, I32)
 
-        size = [sb(f"size{t}", [P, 2 * S], F32) for t in range(PACK)]
-        larger = [size[t][:, S:] for t in range(PACK)]
-        sum_ps = [psum.tile([P, S], F32, name=f"sum_ps{jb}", tag=f"bank{PACK + jb}") for jb in range(PACK)]
+        b_size = sb_rows("b_size", 2 * S)
+        larger = [b_size[t][:, S:] for t in range(PACK)]
+        z2_sum_ps = banks("z2_sum_ps", PACK)
 
-        def add_turned(banks, t, *terms):
+        def add_turned(sums, t, *terms):
             for jb in range(PACK):
                 for i, term in enumerate(terms):
                     nc.tensor.matmul(
-                        banks[jb][:, P * t : P * (t + 1)], lhsT=term[:, P * jb : P * (jb + 1)], rhs=ident[:],
+                        sums[jb][:, block(t)], lhsT=term[:, block(jb)], rhs=ident[:],
                         start=i == 0, stop=i == len(terms) - 1, is_transpose=True,
                     )
 
-        for t in range(PACK + 1):
-            if t < PACK:
-                nc.vector.tensor_tensor(larger[t], g6[t][:], g7[t][:], ALU.min if t in N5_TILES else ALU.max)
-            if 0 < t <= YS_ON_VECTOR:
-                nc.vector.tensor_scalar(ys[t - 1][:, :S], y[t - 1][:, :S], gs34[:, t - 1 : t], None, ALU.mult)
-            if t in N5_TILES:
-                add_turned(sum_ps, t, y[t], diff[t], larger[t])
-            elif t < PACK:
-                nc.vector.tensor_tensor(diff[t][:], y[t][:].indirect(n5_l[:]), larger[t], ALU.subtract)
-                add_turned(sum_ps, t, y[t], diff[t])
+        def scale_y(t):
+            nc.vector.tensor_scalar(y_gs[t][:, :S], y[t][:, :S], z_factor[:, t : t + 1], None, ALU.mult)
 
-        def quantized(name):
-            return sb(name + "_bf", [P, S, PACK], BF16), sb(name + "_codes", [P, S], U32), sb(name + "_scales", [P, S], U8)
+        for t in range(PACK):
+            nc.vector.tensor_tensor(larger[t], y_n6[t][:], y_n7[t][:], ALU.min if t == N5_SCALAR_TILE else ALU.max)
+            if t > 0:
+                scale_y(t - 1)
+            if t == N5_SCALAR_TILE:
+                add_turned(z2_sum_ps, t, y[t], z2_term[t], larger[t])
+            else:
+                nc.vector.tensor_tensor(z2_term[t][:], y[t][:].indirect(n5_l[:]), larger[t], ALU.subtract)
+                add_turned(z2_sum_ps, t, y[t], z2_term[t])
+        scale_y(PACK - 1)
 
-        def quantize(tiles, h):
-            bf, codes, scales = tiles
-            nc.vector.quantize_mx(
-                codes[:, cols(h)].bitcast(FP8X4), scales[:, cols(h)],
-                bf[:, cols(h), :].rearrange("p c t -> p (c t)"),
-            )
+        z2_codes = sb("z2_codes", [P, S], U32)
+        z2_scales = sb("z2_scales", [P, S], U8)
+        y_n1 = sb_rows("y_n1_", S)
+        y_n3 = sb_rows("y_n3_", S)
+        products = sb("products", [P, PACK, 2, S], F32)
+        for t in range(PACK):
+            nc.scalar.activation(y_n1[t][:], y_gs[t][:].indirect(n1_l[:]), ACT.Copy)
+            nc.scalar.activation(y_n3[t][:], y_gs[t][:].indirect(n3_l[:]), ACT.Copy)
 
-        z2_q = quantized("z2")
+        def z_product(t, which):
+            offsets, other = ((n2_l, y_n1), (n4_l, y_n3))[which]
+            nc.vector.tensor_tensor(products[:, t, which, :], y[t][:].indirect(offsets[:]), other[t][:], ALU.mult)
+
+        z_product(0, 0)
         z2_turned = [sb(f"z2_turned{jb}", [P, 2, P, 2], BF16) for jb in range(PACK)]
         pairs_ps = [psum.tile([P, 2, 2, P], F32, name=f"pairs_ps{h}", tag=f"bank{h}") for h in range(2)]
         for jb in range(PACK):
             nc.vector.tensor_tensor(
                 z2_turned[jb][:],
-                sum_ps[jb][:].rearrange("j (u e p) -> j u p e", u=2, e=2),
+                z2_sum_ps[jb][:].rearrange("j (u e p) -> j u p e", u=2, e=2),
                 gk_row[:].rearrange("j (p u e) -> j u p e", u=2, e=2),
                 ALU.mult,
             )
-            words = z2_turned[jb][:].rearrange("j u p e -> j (u p e)").bitcast(F32)
+            pairs = z2_turned[jb][:].rearrange("j u p e -> j (u p e)").bitcast(F32)
             for u in range(2):
-                nc.tensor.transpose(pairs_ps[jb // 2][:, jb % 2, u, :], words[:, P * u : P * (u + 1)], ident[:])
-        for h in range(2):
-            z2_pairs = z2_q[0][:, cols(h), :].rearrange("p c t -> p (c t)").bitcast(F32).rearrange("p (b j u) -> p b j u", b=2, u=2)
-            if h < PAIRS_ON_SCALAR:
-                nc.scalar.copy(z2_pairs, pairs_ps[h][:].rearrange("p b u j -> p b j u"))
-            else:
-                nc.vector.tensor_copy(z2_pairs, pairs_ps[h][:].rearrange("p b u j -> p b j u"))
-        for h in range(2):
-            quantize(z2_q, h)
+                nc.tensor.transpose(pairs_ps[jb // 2][:, jb % 2, u, :], pairs[:, block(u)], ident[:])
+        z_product(0, 1)
 
-        b_ps = [psum.tile([P, S], F32, name=f"b_ps{t}", tag=f"bank{PACK + t}") for t in range(PACK)]
-        for t in range(PACK):
-            nc.tensor.matmul_mx(
-                b_ps[t][:],
-                lhsT=key_words[:, P * t : P * (t + 1)].bitcast(FP8X4),
-                lhsT_scale=key_scales[:, P * t : P * (t + 1)],
-                rhs=z2_q[1][:].bitcast(FP8X4),
-                rhs_scale=z2_q[2][:],
-                start=True, stop=True,
+        pieces = ((0, 2), (2, 3), (3, 4))
+        staged = []
+        for i, (lo, hi) in enumerate(pieces):
+            width = 2 * P * (hi - lo)
+            border = (2 * (i + 1) + 1) * S
+            staged.append(products[:].rearrange("p t w c -> p (t w c)")[:, border - width // 2 : border + width // 2])
+            nc.vector.tensor_copy(
+                staged[i].rearrange("p (b j u) -> p b j u", j=P, u=2),
+                pairs_ps[lo // 2][:, lo % 2 : lo % 2 + hi - lo, :, :].rearrange("p b u j -> p b j u"),
+            )
+        for i, (lo, hi) in enumerate(pieces):
+            nc.vector.quantize_mx(
+                z2_codes[:, P * lo : P * hi].bitcast(FP8X4), z2_scales[:, P * lo : P * hi], staged[i].bitcast(BF16)
             )
 
-        g1 = [sb(f"g1_{t}", [P, S], F32) for t in range(PACK)]
-        g3 = [sb(f"g3_{t}", [P, S], F32) for t in range(PACK)]
-        prod12 = sb("prod12", [P, PACK, S], F32)
-        prod34 = sb("prod34", [P, PACK, S], F32)
+        b_ps = banks("b_ps", PACK)
         for t in range(PACK):
-            if t >= YS_ON_VECTOR:
-                nc.scalar.activation(ys[t][:, :S], y_ps[t][:], ACT.Copy, scale=gs34[:, t : t + 1])
-            nc.scalar.activation(g1[t][:], ys[t][:].indirect(n1_l[:]), ACT.Copy)
-            nc.scalar.activation(g3[t][:], ys[t][:].indirect(n3_l[:]), ACT.Copy)
-            nc.vector.tensor_tensor(prod12[:, t, :], y[t][:].indirect(n2_l[:]), g1[t][:], ALU.mult)
-            if t < PACK - N4_ON_SCALAR:
-                nc.vector.tensor_tensor(prod34[:, t, :], y[t][:].indirect(n4_l[:]), g3[t][:], ALU.mult)
-            else:
-                g4 = sb(f"g4_{t}", [P, S], F32)
-                nc.scalar.activation(g4[:], y[t][:].indirect(n4_l[:]), ACT.Copy)
-                nc.vector.tensor_tensor(prod34[:, t, :], g4[:], g3[t][:], ALU.mult)
+            mx_product(b_ps[t][:], key_words[:, block(t)], FP8X4, key_scales[:, block(t)], z2_codes[:], z2_scales[:])
 
-        g9 = [sb(f"g9_{t}", [P, S], F32) for t in range(PACK)]
-        root = [sb(f"root{t}", [P, S], F32) for t in range(PACK)]
-        inv = [sb(f"inv{t}", [P, S], F32) for t in range(PACK)]
-        den_ps = [psum.tile([P, S], F32, name=f"den_ps{jb}", tag=f"bank{jb}") for jb in range(PACK)]
+        for t in range(1, PACK):
+            for which in range(2):
+                z_product(t, which)
+
+        b_n9 = sb_rows("b_n9_", S)
+        root = sb_rows("root", S)
+        inverse_turned = sb_rows("inverse_turned", S)
+        den_ps = banks("den_ps", 0)
         for t in range(PACK):
-            nc.scalar.activation(size[t][:, :S], b_ps[t][:], ACT.Abs, scale=0.0625)
-            nc.scalar.activation(g9[t][:], size[t][:].indirect(n9_l[:]), ACT.Copy)
-            add_turned(den_ps, t, size[t], g9[t])
-        z_q = quantized("z")
+            nc.scalar.activation(b_size[t][:, :S], b_ps[t][:], ACT.Abs, scale=SCORE_SCALE)
+            nc.scalar.activation(b_n9[t][:], b_size[t][:].indirect(n9_l[:]), ACT.Copy)
+            add_turned(den_ps, t, b_size[t], b_n9[t])
+
+        def quantised_tiles(name):
+            return sb(name + "_bf", [P, S, PACK], BF16), sb(name + "_codes", [P, S], U32), sb(name + "_scales", [P, S], U8)
+
+        def quantise_half(bf, codes, scales, h):
+            nc.vector.quantize_mx(
+                codes[:, cols(h)].bitcast(FP8X4), scales[:, cols(h)], bf[:, cols(h), :].rearrange("p c t -> p (c t)")
+            )
+
+        z_bf, z_codes, z_scales = quantised_tiles("z")
         for h in range(2):
             nc.vector.tensor_tensor(
-                woven(z_q[0][:, cols(h), :]), by_rows(prod12[:, :, cols(h)]), by_rows(prod34[:, :, cols(h)]), ALU.subtract
+                woven(z_bf[:, cols(h), :]), by_rows(products[:, :, 0, cols(h)]), by_rows(products[:, :, 1, cols(h)]),
+                ALU.subtract,
             )
         for h in range(2):
-            quantize(z_q, h)
+            quantise_half(z_bf, z_codes, z_scales, h)
 
-        a_ps = [psum.tile([P, S], F32, name=f"a_ps{t}", tag=f"bank{PACK + t}") for t in range(PACK)]
+        a_ps = banks("a_ps", PACK)
         for t in range(PACK):
             for h in range(2):
-                nc.tensor.matmul_mx(
-                    a_ps[t][:, cols(h)],
-                    lhsT=cand_words[:, P * t : P * (t + 1)].bitcast(FP8X4),
-                    lhsT_scale=cand_scales[:, P * t : P * (t + 1)],
-                    rhs=z_q[1][:, cols(h)].bitcast(FP8X4),
-                    rhs_scale=z_q[2][:, cols(h)],
-                    start=True, stop=True,
+                mx_product(
+                    a_ps[t][:, cols(h)], cand_words[:, block(t)], FP8X4, cand_scales[:, block(t)],
+                    z_codes[:, cols(h)], z_scales[:, cols(h)],
                 )
 
-        inv_ps = {}
+        inverse_ps = {}
 
-        def inverse(jb):
-            nc.scalar.activation(root[jb][:], den_ps[jb][:], ACT.Abs_reciprocal_sqrt, bias=half_col[:])
-            if jb < SQ_ON_SCALAR:
-                nc.scalar.activation(inv[jb][:], root[jb][:], ACT.Square)
+        def invert(jb):
+            nc.scalar.activation(root[jb][:], den_ps[jb][:], ACT.Abs_reciprocal_sqrt, bias=one_half[:])
+            if jb < SQUARES_ON_SCALAR:
+                nc.scalar.activation(inverse_turned[jb][:], root[jb][:], ACT.Square)
             else:
-                nc.vector.tensor_tensor(inv[jb][:], root[jb][:], root[jb][:], ALU.mult)
+                nc.vector.tensor_tensor(inverse_turned[jb][:], root[jb][:], root[jb][:], ALU.mult)
             if jb % 2 == 1:
                 h = jb // 2
                 for pair in range(2):
-                    inv_ps[h, pair] = psum.tile([P, 2, HALF], F32, name=f"inv_ps{h}{pair}", tag=f"bank{2 * h + pair}")
+                    bank = psum.tile([P, 2, HALF], F32, name=f"inverse_ps{h}{pair}", tag=f"bank{2 * h + pair}")
+                    inverse_ps[h, pair] = bank
                     for t in (2 * pair, 2 * pair + 1):
                         for u in range(2):
-                            nc.tensor.transpose(
-                                inv_ps[h, pair][:, t % 2, P * u : P * (u + 1)], inv[2 * h + u][:, P * t : P * (t + 1)], ident[:]
-                            )
+                            nc.tensor.transpose(bank[:, t % 2, block(u)], inverse_turned[2 * h + u][:, block(t)], ident[:])
 
-        for jb in range(EARLY_ROOT):
-            inverse(jb)
+        invert(0)
+        invert(1)
 
-        a = [sb(f"a{t}", [P, S], F32) for t in range(PACK)]
-        g8 = [sb(f"g8_{t}", [P, S], F32) for t in range(PACK)]
-        num = [sb(f"num{t}", [P, S], F32) for t in range(PACK)]
-        res = [sb(f"res{h}", [P, PACK, HALF], F32) for h in range(2)]
-        out_q = quantized("out")
+        a = sb_rows("a", S)
+        a_n8 = sb_rows("a_n8_", S)
+        num = sb_rows("num", S)
+        result = [sb(f"result{h}", [P, PACK, HALF], F32) for h in range(2)]
+        out_bf, out_codes, out_scales = quantised_tiles("out")
         out_rows = out_0.rearrange("(p t) j -> p t j", t=PACK)
         out_words = out_1[0].rearrange("p c r -> p (c r)").bitcast(I32)
-        for t in range(A_ON_VECTOR):
-            nc.vector.tensor_scalar(a[t][:], a_ps[t][:], 0.0625, None, ALU.mult)
+        for t in range(A_TILES_ON_VECTOR):
+            nc.vector.tensor_scalar(a[t][:], a_ps[t][:], SCORE_SCALE, None, ALU.mult)
+
+        def numerator(h, t):
+            if h == 0 and t >= A_TILES_ON_VECTOR:
+                nc.scalar.activation(a[t][:], a_ps[t][:], ACT.Copy, scale=SCORE_SCALE)
+            offsets = n8_l[:, h * (HALF // GROUP) : (h + 1) * (HALF // GROUP)]
+            nc.scalar.activation(a_n8[t][:, cols(h)], a[t][:].indirect(offsets), ACT.Copy)
+            if h == 0 and t < 2:
+                invert(2 + t)
+            nc.vector.tensor_tensor(num[t][:, cols(h)], a[t][:, cols(h)], a_n8[t][:, cols(h)], ALU.subtract)
+
+        def quotient(h, t):
+            nc.vector.tensor_tensor(result[h][:, t, :], num[t][:, cols(h)], inverse_ps[h, t // 2][:, t % 2, :], ALU.mult)
+            if t % 2 == 1:
+                nc.sync.dma_start(out_rows[:, t - 1 : t + 1, cols(h)], result[h][:, t - 1 : t + 1, :])
+
+        def store_codes(h):
+            quantise_half(out_bf, out_codes, out_scales, h)
+            nc.sync.dma_start(out_words[:, cols(h)], out_codes[:, cols(h)].bitcast(I32))
+
         steps = [(h, t) for h in range(2) for t in range(PACK)]
+        numerator(*steps[0])
+        for before, step in zip(steps, steps[1:]):
+            numerator(*step)
+            quotient(*before)
+        nc.scalar.copy(woven(out_bf[:, cols(0), :]), by_rows(result[0][:]))
+        quotient(*steps[-1])
+        store_codes(0)
+        nc.vector.tensor_copy(woven(out_bf[:, cols(1), :]), by_rows(result[1][:]))
+        store_codes(1)
 
-        def finish_half(h):
-            quantize(out_q, h)
-            nc.sync.dma_start(out_words[:, cols(h)], out_q[1][:, cols(h)].bitcast(I32))
-
-        for i in range(len(steps) + 1):
-            if i < len(steps):
-                h, t = steps[i]
-                if h == 0 and t >= A_ON_VECTOR:
-                    nc.scalar.activation(a[t][:], a_ps[t][:], ACT.Copy, scale=0.0625)
-                nc.scalar.activation(g8[t][:, cols(h)], a[t][:].indirect(half_list(n8_l, h)), ACT.Copy)
-                if EARLY_ROOT + i < PACK:
-                    inverse(EARLY_ROOT + i)
-                nc.vector.tensor_tensor(num[t][:, cols(h)], a[t][:, cols(h)], g8[t][:, cols(h)], ALU.subtract)
-            if i == PACK + 2 and not WEAVE0_ON_SCALAR:
-                finish_half(0)
-            if i > 0:
-                h, t = steps[i - 1]
-                nc.vector.tensor_tensor(res[h][:, t, :], num[t][:, cols(h)], inv_ps[h, t // 2][:, t % 2, :], ALU.mult)
-                if t % 2 == 1:
-                    nc.sync.dma_start(out_rows[:, t - 1 : t + 1, cols(h)], res[h][:, t - 1 : t + 1, :])
-            if i == PACK + 1 and not WEAVE0_ON_SCALAR:
-                nc.vector.tensor_copy(woven(out_q[0][:, cols(0), :]), by_rows(res[0][:]))
-            if i == 2 * PACK - 1 and WEAVE0_ON_SCALAR:
-                nc.scalar.copy(woven(out_q[0][:, cols(0), :]), by_rows(res[0][:]))
-        if WEAVE0_ON_SCALAR:
-            finish_half(0)
-        nc.vector.tensor_copy(woven(out_q[0][:, cols(1), :]), by_rows(res[1][:]))
-        finish_half(1)
         out_scale_rows = out_2[0].bitcast(I32)
-        for q in range(4):
+        for q in range(P // QUAD):
             queue = nc.sync if q % 2 == 0 else nc.scalar
-            queue.dma_start(out_scale_rows[4 * q : 4 * q + 4, :], out_q[2][32 * q : 32 * q + 4, :].bitcast(I32))
+            queue.dma_start(
+                out_scale_rows[PACK * q : PACK * (q + 1), :], out_scales[QUAD * q : QUAD * q + PACK, :].bitcast(I32)
+            )

@@ -90,8 +90,6 @@ def tile_picked_cdkeynormbdettrim_none_po_kernel(
         y = sb_rows("y", 2 * S)
         y_gs = sb_rows("y_gs", S + SPARE)
 
-        warm = sb("warm", [P, 2], F32)
-        nc.vector.memset(warm[:, 0:1], 1.0)
         nc.vector.memset(key_scales[:].bitcast(I32), 0)
         for t in range(PACK):
             nc.vector.memset(y[t][:, S:], 0.0)
@@ -103,7 +101,6 @@ def tile_picked_cdkeynormbdettrim_none_po_kernel(
         load_quadrant_scales(x_s, x_scales)
         load_words(x_w, x_words)
         load_quadrant_scales(w1_s, w1_scales)
-        nc.scalar.activation(warm[:, 1:2], warm[:, 0:1], ACT.Abs_reciprocal_sqrt)
         cand_l = load_list("cand_l", cand)
         n6_l = load_list("n6_l", n6)
         n7_l = load_list("n7_l", n7)

from contextlib import ExitStack

import concourse.mybir as mybir
from concourse.masks import make_identity

F32 = mybir.dt.float32
BF16 = mybir.dt.bfloat16
I32 = mybir.dt.int32
U32 = mybir.dt.uint32
U16 = mybir.dt.uint16
U8 = mybir.dt.uint8
FP8X4 = mybir.dt.float8_e4m3fn_x4
FP4X4 = mybir.dt.float4_e2m1fn_x4
ALU = mybir.AluOpType
ACT = mybir.ActivationFunctionType

P = 128
PACK = 4
S = 512
T = 1024
G = 2048
HALF = S // 2
GROUP = 16
QUAD = 32
BLOCK_PARTS = 8
SPARE = 16
SCORE_SCALE = 0.0625

N5_SCALAR_TILE = 3
SQUARES_ON_SCALAR = 1
A_TILES_ON_VECTOR = 3

FLOPS = 3 * 2 * S * S * S


def tile_picked_cdkeynormbdettrim_none_po_kernel(
    tc, x_words, x_scales, w1_words, w1_scales, gs, gk, d_words, d_scales,
    offs, n1, n2, n3, n4, n5, n6, n7, cand, k1, n8, n9, out_0, out_1, out_2,
):
    nc = tc.nc
    with ExitStack() as ctx:
        pool = ctx.enter_context(tc.tile_pool(name="keep", bufs=1))
        psum = ctx.enter_context(tc.psum_pool(name="psum", bufs=1))

        def sb(name, shape, dtype):
            return pool.tile(shape, dtype, name=name, align_bytes=64)

        def sb_rows(name, width):
            return [sb(f"{name}{t}", [P, width], F32) for t in range(PACK)]

        def banks(name, first):
            return [psum.tile([P, S], F32, name=f"{name}{t}", tag=f"bank{first + t}") for t in range(PACK)]

        def load_list(name, dram):
            tile = sb(name, [P, S // GROUP], U16)
            nc.sync.dma_start(tile[:], dram)
            return tile

        def load_words(tile, dram):
            nc.sync.dma_start(tile[:], dram[0].rearrange("p c r -> p (c r)").bitcast(I32))

        def load_quadrant_scales(tile, dram):
            rows = dram[0].bitcast(I32)
            for q in range(P // QUAD):
                four = rows[PACK * q : PACK * (q + 1), :]
                nc.sync.dma_start(
                    tile[QUAD * q : QUAD * (q + 1), :].bitcast(I32),
                    four.unsqueeze(0).to_broadcast([QUAD // PACK, PACK, four.shape[1]]),
                )

        def cols(h):
            return slice(h * HALF, (h + 1) * HALF)

        def block(i):
            return slice(P * i, P * (i + 1))

        def woven(tile):
            return tile.rearrange("p (c i) t -> p c t i", i=4)

        def by_rows(tile):
            return tile.rearrange("p t (c i) -> p c t i", i=4)

        x_w = sb("x_w", [P, T], I32)
        x_s = sb("x_s", [P, T], U8)
        w1_w = sb("w1_w", [P, 2 * S], U8)
        w1_s = sb("w1_s", [P, S], U8)
        d_w = sb("d_w", [P, G], I32)
        d_s = sb("d_s", [P, G], U8)
        key_scales = sb("key_scales", [P, S], U8)
        y = sb_rows("y", 2 * S)
        y_gs = sb_rows("y_gs", S + SPARE)

        nc.vector.memset(key_scales[:].bitcast(I32), 0)
        for t in range(PACK):
            nc.vector.memset(y[t][:, S:], 0.0)
        for t in range(PACK):
            nc.vector.memset(y_gs[t][:, S:], 0.0)

        offs_l = load_list("offs_l", offs)
        nc.sync.dma_start(w1_w[:].bitcast(I32), w1_words[0].bitcast(I32))
        load_quadrant_scales(x_s, x_scales)
        load_words(x_w, x_words)
        load_quadrant_scales(w1_s, w1_scales)
        cand_l = load_list("cand_l", cand)
        n6_l = load_list("n6_l", n6)
        n7_l = load_list("n7_l", n7)
        load_words(d_w, d_words)
        k1_l = load_list("k1_l", k1)
        nc.sync.dma_start(
            d_s[:].bitcast(I32),
            d_scales[0].bitcast(I32).unsqueeze(1).to_broadcast([P // BLOCK_PARTS, BLOCK_PARTS, G // 4]),
        )
        n5_l = load_list("n5_l", n5)
        gs_rows = sb("gs_rows", [P, PACK], F32)
        nc.sync.dma_start(gs_rows[:], gs.rearrange("(p t) o -> p (t o)", t=PACK))
        n1_l = load_list("n1_l", n1)
        n3_l = load_list("n3_l", n3)
        n2_l = load_list("n2_l", n2)
        n4_l = load_list("n4_l", n4)
        n9_l = load_list("n9_l", n9)
        n8_l = load_list("n8_l", n8)
        gk_row = sb("gk_row", [P, S], F32)
        nc.sync.dma_start(gk_row[:], gk.rearrange("k o -> o k").to_broadcast([P, S]))

        ident = sb("ident", [P, P], F32)
        make_identity(nc, ident[:])
        one_half = sb("one_half", [P, 1], F32)
        nc.vector.memset(one_half[:], 0.5)
        z_factor = sb("z_factor", [P, PACK], F32)
        nc.gpsimd.tensor_scalar(z_factor[:], gs_rows[:], 0.75, 0.0, ALU.mult, ALU.add)

        def gather_packed(name, window, dtype, offsets):
            picked = sb(name, [P, S], dtype)
            nc.vector.tensor_copy(picked[:], window[:].bitcast(dtype).indirect(offsets[:]))
            return picked

        def deal(dst, src, tiles=slice(0, PACK)):
            nc.vector.tensor_copy(
                dst.rearrange("p (t m) -> p m t", t=PACK)[:, :, tiles],
                src.rearrange("p (m t) -> p m t", t=PACK)[:, :, tiles],
            )

        def dealt(name, src, dtype):
            dst = sb(name, [P, S], dtype)
            deal(dst[:], src[:].bitcast(dtype))
            return dst

        def mx_product(out, words, words_dtype, scales, codes, code_scales):
            nc.tensor.matmul_mx(
                out, lhsT=words.bitcast(words_dtype), lhsT_scale=scales,
                rhs=codes.bitcast(FP8X4), rhs_scale=code_scales, start=True, stop=True,
            )

        w_words = sb("w_words", [P, 2 * S], U8)
        w_scales = sb("w_scales", [P, S], U8)
        deal(w_words[:].bitcast(U16), w1_w[:].bitcast(U16))
        xq_scales = gather_packed("xq_scales", x_s, U8, offs_l)
        xq_words = gather_packed("xq_words", x_w, U32, offs_l)
        deal(w_scales[:], w1_s[:], slice(0, 1))
        deal(w_scales[:], w1_s[:], slice(1, PACK))

        y_ps = banks("y_ps", 0)
        for t in range(PACK):
            mx_product(
                y_ps[t][:], w_words[:, 2 * P * t : 2 * P * (t + 1)], FP4X4, w_scales[:, block(t)], xq_words[:], xq_scales[:]
            )

        y_n6 = sb_rows("y_n6_", S)
        z2_term = sb_rows("z2_term", S)
        y_n7 = sb_rows("y_n7_", S)
        for t in range(PACK):
            nc.scalar.copy(y[t][:, :S], y_ps[t][:])
            sign = -1.0 if t == N5_SCALAR_TILE else 1.0
            nc.scalar.activation(y_n6[t][:], y[t][:].indirect(n6_l[:]), ACT.Copy, scale=sign)
            nc.scalar.activation(y_n7[t][:], y[t][:].indirect(n7_l[:]), ACT.Copy, scale=sign)
            if t == N5_SCALAR_TILE:
                nc.scalar.activation(z2_term[t][:], y[t][:].indirect(n5_l[:]), ACT.Copy)

        cand_picked_words = gather_packed("cand_picked_words", x_w, U32, cand_l)
        cand_picked_scales = gather_packed("cand_picked_scales", x_s, U8, cand_l)
        key_picked_scales = gather_packed("key_picked_scales", d_s, U8, k1_l)
        key_picked_words = gather_packed("key_picked_words", d_w, U32, k1_l)
        key_dealt_scales = dealt("key_dealt_scales", key_picked_scales, U8)
        for r in range(PACK):
            nc.sync.dma_start(
                key_scales[r:P:QUAD, :].bitcast(I32), key_dealt_scales[BLOCK_PARTS * r : P : QUAD, :].bitcast(I32)
            )
        cand_words = dealt("cand_words", cand_picked_words, I32)
        cand_scales = dealt("cand_scales", cand_picked_scales, U8)
        key_words = dealt("key_words", key_picked_words, I32)

        b_size = sb_rows("b_size", 2 * S)
        larger = [b_size[t][:, S:] for t in range(PACK)]
        z2_sum_ps = banks("z2_sum_ps", PACK)

        def add_turned(sums, t, *terms):
            for jb in range(PACK):
                for i, term in enumerate(terms):
                    nc.tensor.matmul(
                        sums[jb][:, block(t)], lhsT=term[:, block(jb)], rhs=ident[:],
                        start=i == 0, stop=i == len(terms) - 1, is_transpose=True,
                    )

        def scale_y(t):
            nc.vector.tensor_scalar(y_gs[t][:, :S], y[t][:, :S], z_factor[:, t : t + 1], None, ALU.mult)

        for t in range(PACK):
            nc.vector.tensor_tensor(larger[t], y_n6[t][:], y_n7[t][:], ALU.min if t == N5_SCALAR_TILE else ALU.max)
            if t > 0:
                scale_y(t - 1)
            if t == N5_SCALAR_TILE:
                add_turned(z2_sum_ps, t, y[t], z2_term[t], larger[t])
            else:
                nc.vector.tensor_tensor(z2_term[t][:], y[t][:].indirect(n5_l[:]), larger[t], ALU.subtract)
                add_turned(z2_sum_ps, t, y[t], z2_term[t])
        scale_y(PACK - 1)

        z2_codes = sb("z2_codes", [P, S], U32)
        z2_scales = sb("z2_scales", [P, S], U8)
        y_n1 = sb_rows("y_n1_", S)
        y_n3 = sb_rows("y_n3_", S)
        products = sb("products", [P, PACK, 2, S], F32)
        for t in range(PACK):
            nc.scalar.activation(y_n1[t][:], y_gs[t][:].indirect(n1_l[:]), ACT.Copy)
            nc.scalar.activation(y_n3[t][:], y_gs[t][:].indirect(n3_l[:]), ACT.Copy)

        def z_product(t, which):
            offsets, other = ((n2_l, y_n1), (n4_l, y_n3))[which]
            nc.vector.tensor_tensor(products[:, t, which, :], y[t][:].indirect(offsets[:]), other[t][:], ALU.mult)

        z_product(0, 0)
        z2_turned = [sb(f"z2_turned{jb}", [P, 2, P, 2], BF16) for jb in range(PACK)]
        pairs_ps = [psum.tile([P, 2, 2, P], F32, name=f"pairs_ps{h}", tag=f"bank{h}") for h in range(2)]
        for jb in range(PACK):
            nc.vector.tensor_tensor(
                z2_turned[jb][:],
                z2_sum_ps[jb][:].rearrange("j (u e p) -> j u p e", u=2, e=2),
                gk_row[:].rearrange("j (p u e) -> j u p e", u=2, e=2),
                ALU.mult,
            )
            pairs = z2_turned[jb][:].rearrange("j u p e -> j (u p e)").bitcast(F32)
            for u in range(2):
                nc.tensor.transpose(pairs_ps[jb // 2][:, jb % 2, u, :], pairs[:, block(u)], ident[:])
        z_product(0, 1)

        pieces = ((0, 2), (2, 3), (3, 4))
        staged = []
        for i, (lo, hi) in enumerate(pieces):
            width = 2 * P * (hi - lo)
            border = (2 * (i + 1) + 1) * S
            staged.append(products[:].rearrange("p t w c -> p (t w c)")[:, border - width // 2 : border + width // 2])
            nc.vector.tensor_copy(
                staged[i].rearrange("p (b j u) -> p b j u", j=P, u=2),
                pairs_ps[lo // 2][:, lo % 2 : lo % 2 + hi - lo, :, :].rearrange("p b u j -> p b j u"),
            )
        for i, (lo, hi) in enumerate(pieces):
            nc.vector.quantize_mx(
                z2_codes[:, P * lo : P * hi].bitcast(FP8X4), z2_scales[:, P * lo : P * hi], staged[i].bitcast(BF16)
            )

        b_ps = banks("b_ps", PACK)
        for t in range(PACK):
            mx_product(b_ps[t][:], key_words[:, block(t)], FP8X4, key_scales[:, block(t)], z2_codes[:], z2_scales[:])

        for t in range(1, PACK):
            for which in range(2):
                z_product(t, which)

        b_n9 = sb_rows("b_n9_", S)
        root = sb_rows("root", S)
        inverse_turned = sb_rows("inverse_turned", S)
        den_ps = banks("den_ps", 0)
        for t in range(PACK):
            nc.scalar.activation(b_size[t][:, :S], b_ps[t][:], ACT.Abs, scale=SCORE_SCALE)
            nc.scalar.activation(b_n9[t][:], b_size[t][:].indirect(n9_l[:]), ACT.Copy)
            add_turned(den_ps, t, b_size[t], b_n9[t])

        def quantised_tiles(name):
            return sb(name + "_bf", [P, S, PACK], BF16), sb(name + "_codes", [P, S], U32), sb(name + "_scales", [P, S], U8)

        def quantise_half(bf, codes, scales, h):
            nc.vector.quantize_mx(
                codes[:, cols(h)].bitcast(FP8X4), scales[:, cols(h)], bf[:, cols(h), :].rearrange("p c t -> p (c t)")
            )

        z_bf, z_codes, z_scales = quantised_tiles("z")
        for h in range(2):
            nc.vector.tensor_tensor(
                woven(z_bf[:, cols(h), :]), by_rows(products[:, :, 0, cols(h)]), by_rows(products[:, :, 1, cols(h)]),
                ALU.subtract,
            )
        for h in range(2):
            quantise_half(z_bf, z_codes, z_scales, h)

        a_ps = banks("a_ps", PACK)
        for t in range(PACK):
            for h in range(2):
                mx_product(
                    a_ps[t][:, cols(h)], cand_words[:, block(t)], FP8X4, cand_scales[:, block(t)],
                    z_codes[:, cols(h)], z_scales[:, cols(h)],
                )

        inverse_ps = {}

        def invert(jb):
            nc.scalar.activation(root[jb][:], den_ps[jb][:], ACT.Abs_reciprocal_sqrt, bias=one_half[:])
            if jb < SQUARES_ON_SCALAR:
                nc.scalar.activation(inverse_turned[jb][:], root[jb][:], ACT.Square)
            else:
                nc.vector.tensor_tensor(inverse_turned[jb][:], root[jb][:], root[jb][:], ALU.mult)
            if jb % 2 == 1:
                h = jb // 2
                for pair in range(2):
                    bank = psum.tile([P, 2, HALF], F32, name=f"inverse_ps{h}{pair}", tag=f"bank{2 * h + pair}")
                    inverse_ps[h, pair] = bank
                    for t in (2 * pair, 2 * pair + 1):
                        for u in range(2):
                            nc.tensor.transpose(bank[:, t % 2, block(u)], inverse_turned[2 * h + u][:, block(t)], ident[:])

        invert(0)
        invert(1)

        a = sb_rows("a", S)
        a_n8 = sb_rows("a_n8_", S)
        num = sb_rows("num", S)
        result = [sb(f"result{h}", [P, PACK, HALF], F32) for h in range(2)]
        out_bf, out_codes, out_scales = quantised_tiles("out")
        out_rows = out_0.rearrange("(p t) j -> p t j", t=PACK)
        out_words = out_1[0].rearrange("p c r -> p (c r)").bitcast(I32)
        for t in range(A_TILES_ON_VECTOR):
            nc.vector.tensor_scalar(a[t][:], a_ps[t][:], SCORE_SCALE, None, ALU.mult)

        def numerator(h, t):
            if h == 0 and t >= A_TILES_ON_VECTOR:
                nc.scalar.activation(a[t][:], a_ps[t][:], ACT.Copy, scale=SCORE_SCALE)
            offsets = n8_l[:, h * (HALF // GROUP) : (h + 1) * (HALF // GROUP)]
            nc.scalar.activation(a_n8[t][:, cols(h)], a[t][:].indirect(offsets), ACT.Copy)
            if h == 0 and t < 2:
                invert(2 + t)
            nc.vector.tensor_tensor(num[t][:, cols(h)], a[t][:, cols(h)], a_n8[t][:, cols(h)], ALU.subtract)

        def quotient(h, t):
            nc.vector.tensor_tensor(result[h][:, t, :], num[t][:, cols(h)], inverse_ps[h, t // 2][:, t % 2, :], ALU.mult)
            if t % 2 == 1:
                nc.sync.dma_start(out_rows[:, t - 1 : t + 1, cols(h)], result[h][:, t - 1 : t + 1, :])

        def store_codes(h):
            quantise_half(out_bf, out_codes, out_scales, h)
            nc.sync.dma_start(out_words[:, cols(h)], out_codes[:, cols(h)].bitcast(I32))

        steps = [(h, t) for h in range(2) for t in range(PACK)]
        numerator(*steps[0])
        for before, step in zip(steps, steps[1:]):
            numerator(*step)
            quotient(*before)
        nc.scalar.copy(woven(out_bf[:, cols(0), :]), by_rows(result[0][:]))
        quotient(*steps[-1])
        store_codes(0)
        nc.vector.tensor_copy(woven(out_bf[:, cols(1), :]), by_rows(result[1][:]))
        store_codes(1)

        out_scale_rows = out_2[0].bitcast(I32)
        for q in range(P // QUAD):
            queue = nc.sync if q % 2 == 0 else nc.scalar
            queue.dma_start(
                out_scale_rows[PACK * q : PACK * (q + 1), :], out_scales[QUAD * q : QUAD * q + PACK, :].bitcast(I32)
            )
